import numpy as np, ml_dtypes
CORES = [35,38,43,46]
N = 4
BF = ml_dtypes.bfloat16
def gentries(a):
    return np.ascontiguousarray(a.reshape(8, 16, -1).transpose(0, 2, 1)).reshape(8, -1)
def gtable(e):
    e = np.asarray(e); return np.ascontiguousarray(e.reshape(8, -1, 16).transpose(0, 2, 1)).reshape(128, -1).astype(np.int32)
def f(rng, *shape):
    return (rng.standard_normal(shape, dtype=np.float32) * np.exp2(rng.integers(-2, 3, shape[:-1] + (1,)))).astype(BF)
def wide(rng, *shape):
    v = f(rng, *shape).astype(np.float32); k = shape[:-2] + (1, shape[-1])
    return (v * np.exp2(rng.integers(-6, 7, k)) * (rng.random(k) > 0.0625)).astype(BF)
V, D, C, R = 2048, 2, 96, 3
def ranks(t):
    return t.reshape(8, D, N, V).transpose(2, 0, 1, 3)
def globe(a, bl):
    out = np.zeros((N, 8, D * V), np.int64)
    for r in range(N):
        own = np.broadcast_to(r * V + np.arange(V), (8, V))
        ghosts = (np.arange(N)[:, None, None] * V + bl[:, :, r]).transpose(1, 0, 2).reshape(8, N * C)
        out[r] = np.take_along_axis(np.concatenate([own, ghosts], 1), a[r].reshape(8, D * V).astype(np.int64), 1)
    return out.reshape(N, 8, D, V).transpose(1, 2, 0, 3).reshape(8, D, N * V)
def unpack(nb, bl):
    return np.stack([gentries(t) for t in nb]).reshape(N, 8, D, V), np.stack([gentries(t) for t in bl]).reshape(N, 8, N, C)
def pack(rng, a, bl, v):
    o = np.argsort(rng.random(a.shape), 2); a = np.take_along_axis(a, o, 2); v = np.take_along_axis(v, o, 2)
    return {"nb": np.stack([gtable(t.reshape(8, D * V)) for t in a]), "bl": np.stack([gtable(t.reshape(8, N * C)) for t in bl]),
            "w": np.ascontiguousarray(v).reshape(N, 8, D * V).astype(np.float32).astype(BF), "x": f(rng, N, 128, V)}
def graphs(rng, p):
    bl = np.argsort(rng.random((N, 8, N, V)), axis=-1)[..., :C]
    a = np.full((N, 8, D, V), -1, np.int64)
    for g in range(8):
        for d in range(D):
            for r in range(N):
                for q in range(r):
                    o = rng.permutation(C); u = bl[r, g, q]; t = bl[q, g, r][o]
                    k = (a[r, g, d, u] < 0) & (a[q, g, d, t] < 0) & (rng.random(C) < p)
                    a[r, g, d, u[k]] = V + q * C + o[k]; a[q, g, d, t[k]] = V + r * C + np.flatnonzero(k)
            for r in range(N):
                e = rng.permutation(np.flatnonzero(a[r, g, d] < 0)); h = len(e) // 2
                a[r, g, d, e[:h]] = e[h:2 * h]; a[r, g, d, e[h:2 * h]] = e[:h]
                if len(e) > 2 * h: a[r, g, d, e[-1]] = (e[-1] + 1) % V
        for r in range(N):
            alias = np.full(V, -1, np.int64); alias[bl[r, g, r]] = V + r * C + np.arange(C)
            b = a[r, g]; n = np.where(b < V, alias[np.minimum(b, V - 1)], -1)
            a[r, g] = np.where((n >= 0) & (rng.random((D, V)) < 0.5), n, b)
    return a, bl
def both(a, bl, z):
    return np.array(ranks(np.take_along_axis(z, np.minimum(globe(a, bl), np.arange(N * V)), 2)))
def setup_inputs(rng):
    a, bl = graphs(rng, 0.6)
    return pack(rng, a, bl, both(a, bl, np.exp2(4 * rng.random((8, D, N * V)))))
def setup_inputs_ties(rng):
    a, bl = graphs(rng, 0.6); z = rng.integers(1, 4, (8, D, N * V)).astype(np.float64); z[rng.integers(0, 8)] = 1
    z *= np.exp2(rng.integers(-20, 21, (8, 1, 1)))
    return pack(rng, a, bl, both(a, bl, z))
def setup_inputs_borders(rng):
    a, bl = graphs(rng, 1.0); v = both(a, bl, np.exp2(3 * rng.random((8, D, N * V))))
    far = ranks(globe(a, bl) // V != np.arange(N * V) // V)
    return pack(rng, a, bl, v * np.where(far, 8, 1))
def setup_inputs_hubs(rng):
    a, bl = graphs(rng, 0.6); v = both(a, bl, np.exp2(4 * rng.random((8, D, N * V))))
    for r in range(N):
        for g in range(8):
            e = rng.permutation(V); h = e[:16]; leaves = e[16:V // 2]; b = a[r, g]; c = v[r, g]
            b[:, leaves] = h[rng.integers(0, 16, (D, len(leaves)))]
            b[0, h] = h[np.arange(16) ^ 1]; c[0, h] = 256
    return pack(rng, a, bl, v)
def setup_inputs_any(rng):
    bl = rng.integers(0, V, (N, 8, N, C)); bl[..., C // 2:] = bl[..., :1]; bl[..., 1] = 0; bl[..., 2] = V - 1
    a = rng.integers(0, V + N * C, (N, 8, D, V)); j = np.arange(V)
    a = np.where(ranks(globe(a, bl) == np.arange(N * V)), (j + 1) % V, a)
    o = rng.permutation(8); a[:, o[0]] = (j + 1) % V; a[:, o[1]] = j ^ 1
    for r in range(N):
        for g in o[2:5]:
            q = r ^ 1
            a[r, g, :, bl[r, g, q, 0]] = V + q * C + rng.choice(np.r_[0, C // 2:C], D)
    return pack(rng, a, bl, np.exp2(4 * rng.random((N, 8, D, V))))
def setup_inputs_spread(rng):
    a, bl = graphs(rng, 0.6); z = np.exp2(rng.integers(-3, 4, (8, D, N * V)) + rng.random((8, D, N * V)))
    d = pack(rng, a, bl, both(a, bl, z)); d["x"] = wide(rng, N, 128, V); return d
def check_inputs(d):
    bad = []
    if d["bl"].min() < 0 or d["bl"].max() >= V: bad.append("bl")
    if d["nb"].min() < 0 or d["nb"].max() >= V + N * C: bad.append("nb")
    if not bad and (globe(*unpack(d["nb"], d["bl"])) == np.arange(N * V)).any(): bad.append("own neighbour")
    u = d["w"].astype(np.float32)
    if not (np.isfinite(u).all() and (u > 0).all()): bad.append("w")
    v = np.abs(d["x"].astype(np.float32))
    if not np.isfinite(v).all(): bad.append("x")
    if not 4.0 * D * float(u.max()) * float(v.max()) < 2.0 ** 127: bad.append("range")
    return bad
def reference(nb, bl, w, x):
    i = np.arange(N * V); A = globe(*unpack(nb, bl))
    u = w.astype(np.float64).reshape(N, 8, D, V).transpose(1, 2, 0, 3).reshape(8, D, N * V)
    mate = np.tile(i, (8, 1)); free = np.ones((8, N * V), bool)
    for t in range(R):
        k = np.where(np.take_along_axis(free[:, None], A, 2), u, 0.0)
        P = np.take_along_axis(A, np.argmax(k, 1)[:, None], 1)[:, 0]
        P = np.where(free & (np.max(k, 1) > 0), P, -1)
        hit = (P >= 0) & (np.take_along_axis(P, np.maximum(P, 0), 1) == i)
        mate = np.where(hit, P, mate); free = free & ~hit
    two = mate != i; first = np.minimum(mate, i); rep = first == i
    num = (np.add.accumulate(rep.reshape(8, N, V).astype(np.int64), 2) - 1 + V * np.arange(N)[:, None]).reshape(8, N * V)
    cm = np.take_along_axis(num, first, 1).reshape(8, N, V)
    xx = np.ascontiguousarray(x.astype(np.float64).reshape(N, 8, 16, V).transpose(1, 2, 0, 3)).reshape(8, 16, N * V)
    X = xx + np.where(two[:, None], np.take_along_axis(xx, mate[:, None], 2), 0.0)
    s = np.zeros((8, 16, N * V))
    for d in range(D):
        s += u[:, d, None] * np.take_along_axis(X, A[:, d, None], 2)
    s = s + np.where(two[:, None], np.take_along_axis(s, mate[:, None], 2), 0.0)
    y = np.zeros((8, 16, N * V))
    for g in range(8):
        y[g][:, num[g, rep[g]]] = s[g][:, rep[g]]
    y = np.ascontiguousarray(y.reshape(8, 16, N, V).transpose(2, 0, 1, 3)).reshape(N, 128, V)
    return {"y": y.astype(np.float32), "cm": np.stack([gtable(cm[:, r]) for r in range(N)]).astype(np.float32)}

@@ -1,0 +1,515 @@
+import math
+from concourse.bass import DstId, RemoteDMATransfer
+from concourse.mybir import AluOpType, ActivationFunctionType
+
+OP = AluOpType
+AF = ActivationFunctionType
+V, C, Z = 2048, 96, 2432
+F32, BF, I32, U16 = "float32", "bfloat16", "int32", "uint16"
+WIDTHS = {
+    F32: dict(nbf=256, col=128, jr=8, jb=8, ir=128, rg=128, rgam=128, aw=128, ownt=256, ownp=128, iff=128, g8=8, sel1f=8, vl=128,
+              vz=128, w0s=128, dn=128, bd=128, hlf=256, h4=256, l4=256, beta=256, alph=256, stf=512, pif=256, t1=256, xf=2432,
+              xb=384, num=128, cn=128, off=128, ms=128, sp=2432, sb=384, g1=2048, p0=2048, sw=2448, sst=384, id64=2048, inv=4096,
+              ivt=128, gcm=2048, cmt=128, cmv=128, tw=2064, yt=2048),
+    BF: dict(wsb=4096, xw=2448, ia=256, ic=256, nwa=256, nwb=256, ib=128, nib=128, i128=64, blk=128, lt=128, tri=128, samg=128, pack=1024,
+             src=512, lst=64, selg=24, sel4=16, sel1=8, e8=128, nw=2432, bst=384, xst=384, xc=2048, wtb=2, bt=128, gb=8192, rh=256,
+             rh2=256, w0r=2048, sq=512, wm=8192, mq=512, cq=512, zt=128, zl=128, mp=256, mlh=128, ww=1024, pp=256, ar=256, bb=128,
+             nz=128, cd=128, mcode=128, tc=128, rep=128, rt=128, up=128),
+    I32: dict(bli=24, nbi=256, coli=16, li=256, sti=512, lj=256, yi=512, zi=512, ivi=128),
+    U16: dict(bl16=24, nb16=256, hl16=256, pl16=256, idx=512, mate=128, ms16=128, off16=128, iv16=128),
+}
+PSUM = {"psw": 2048, "pa": 512, "pb": 512, "pc": 512, "pd": 512}
+SCRATCH = {"snd": ("sbuf", [128, 4, 128], BF), "tg": ("sbuf", [128, 4, 128], BF)}
+for _d in WIDTHS:
+    for _n in WIDTHS[_d]:
+        SCRATCH[_n] = ("sbuf", [128, WIDTHS[_d][_n]], _d)
+for _n in PSUM:
+    SCRATCH[_n] = ("psum", [128, PSUM[_n]], F32)
+EXCH = ["name", "x", "gid", "code", "xs", "num", "s"]
+LOADS = ["bl", "nb", "w", "x", "xc", "y0", "y1", "y2", "y3", "cm"]
+SEMAPHORES = ["cV", "cS", "cP", "cG"] + ["d_" + k for k in LOADS] + ["a_" + k for k in EXCH] + ["l_" + k for k in EXCH]
+
+
+def engine_plan(topo, src, cores):
+    away = [d for d in cores if d != src and topo.chip(d) != topo.chip(src)]
+    near = [d for d in cores if d != src and topo.chip(d) == topo.chip(src)]
+    used, out = [], {}
+    for group in (away, near):
+        for i, d in enumerate(group):
+            free = [e for e in topo.engines(src, d) if e not in used]
+            n = 1
+            while n * 2 <= len(free) // (len(group) - i) and n < 8:
+                n *= 2
+            out[d] = free[:n]
+            used = used + out[d]
+    return out
+
+
+def rank_program(g, core, T, topo):
+    r = T.rank_of(core)
+    if r is None:
+        return
+    cores = [int(c) for c in T.cores]
+    others = [d for d in range(len(cores)) if d != r]
+    queue = {"V": g.vector, "S": g.scalar, "P": g.tensor, "G": g, "Y": g.sync}
+    total, known, hist = {}, {q: {} for q in queue}, {}
+
+    def deps(q, tag, regs, kind, need):
+        for name, p0, p1, c0, c1 in regs:
+            ps = name in PSUM
+            for o, k, a0, a1, b0, b1 in hist.get(name, ()):
+                cross = ps and o["q"] != q
+                if kind == "r" and k == "r" and not cross:
+                    continue
+                if tag is not None and o["tag"] == tag and o["q"] == q:
+                    continue
+                if cross:
+                    hit = c0 // 512 <= (b1 - 1) // 512 and b0 // 512 <= (c1 - 1) // 512
+                else:
+                    hit = c0 < b1 and b0 < c1 and p0 < a1 and a0 < p1
+                if hit and (o["sem"] not in need or need[o["sem"]]["val"] < o["val"]):
+                    need[o["sem"]] = o
+
+    def note(o, outs, ins):
+        for kind, regs in (("w", outs), ("r", ins)):
+            for name, p0, p1, c0, c1 in regs:
+                hist.setdefault(name, []).append((o, kind, p0, p1, c0, c1))
+
+    def add(q, fn, outs, ins, sem=None, inc=1, tag=None, chain=True):
+        need, kq = {}, known[q]
+        deps(q, tag, ins, "r", need)
+        deps(q, tag, outs, "w", need)
+        for s, o in need.items():
+            if kq.get(s, 0) >= o["val"] or any(p is not o and p["know"].get(s, 0) >= o["val"] for p in need.values()):
+                continue
+            queue[q].wait_ge(T.sem[s], o["val"])
+            for k, v in o["know"].items():
+                kq[k] = max(kq.get(k, 0), v)
+        sem = sem or "c" + q
+        total[sem] = total.get(sem, 0) + inc
+        o = {"q": q if sem == "c" + q else q + sem, "tag": tag, "sem": sem, "val": total[sem], "know": dict(kq)}
+        o["know"][sem] = total[sem]
+        made = fn(queue[q])
+        if chain:
+            made.then_inc(T.sem[sem], inc)
+        note(o, outs, ins)
+
+    def X(name, c0, c1, step=1, p0=0, p1=128):
+        ap = T[name][p0:p1, c0:c1] if step == 1 else T[name][p0:p1, c0:c1:step]
+        return ap, [(name, p0, p1, c0, c1)]
+
+    def X3(name, i0, i1, j0, j1):
+        ap = T[name][:, i0:i1, j0:j1] if i1 - i0 > 1 else T[name][:, i0, j0:j1]
+        return ap, [(name, 0, 128, i0 * 128 + j0, (i1 - 1) * 128 + j1)]
+
+    def IX(win, b, offs, c, d):
+        return T[win][:, 0:b].indirect(T[offs][:, c:d]), [(win, 0, 128, 0, b), (offs, 0, 128, c, d)]
+
+    def col(j, p1=128):
+        return X("col", j, j + 1, 1, 0, p1)
+
+    def sc(s):
+        return s[0] if isinstance(s, tuple) else s
+
+    def rg(*xs):
+        return [y for x in xs if isinstance(x, tuple) for y in x[1]]
+
+    def tt(out, a, b, op, tag=None):
+        add("V", lambda e: e.tensor_tensor(out=out[0], in0=a[0], in1=b[0], op=op), rg(out), rg(a, b), tag=tag)
+
+    def ts(out, a, s1, op0, s2=None, op1=None, tag=None):
+        if op1 is None:
+            f = lambda e: e.tensor_scalar(out=out[0], in0=a[0], scalar1=sc(s1), scalar2=None, op0=op0)
+        else:
+            f = lambda e: e.tensor_scalar(out=out[0], in0=a[0], scalar1=sc(s1), scalar2=sc(s2), op0=op0, op1=op1)
+        add("V", f, rg(out), rg(a, s1, s2), tag=tag)
+
+    def cp(out, a, tag=None):
+        add("V", lambda e: e.tensor_copy(out=out[0], in_=a[0]), rg(out), rg(a), tag=tag)
+
+    def act(out, a, func=AF.Identity, bias=0.0, scale=1.0, tag=None):
+        if isinstance(bias, float) and isinstance(scale, float) and bias == 0.0 and scale == 1.0:
+            f = lambda e: e.activation(out=out[0], in_=a[0], func=func)
+        else:
+            f = lambda e: e.activation(out=out[0], in_=a[0], func=func, bias=sc(bias), scale=sc(scale))
+        add("S", f, rg(out), rg(a, bias, scale), tag=tag)
+
+    def mm(out, lhsT, rhs, start=True, stop=True, tag=None):
+        add("P", lambda e: e.matmul(out=out[0], lhsT=lhsT[0], rhs=rhs[0], start=start, stop=stop), rg(out), rg(lhsT, rhs), tag=tag)
+
+    def iota(out, pattern, base, cm, whole=False):
+        if whole:
+            f = lambda e: e.iota(out[0], pattern, base, cm)
+        else:
+            f = lambda e: e.iota(out[0], pattern, base, cm, allow_small_or_imprecise_dtypes=True)
+        add("G", f, rg(out), [])
+
+    def dma(q, key, out_ap, outs, in_ap, ins):
+        add(q, lambda e: e.dma_start(out=out_ap, in_=in_ap), outs, ins, sem="d_" + key, inc=16)
+
+    plans = {c: engine_plan(topo, c, cores) for c in cores}
+
+    def send(key, src, dst):
+        parts, regs, n = [], [], 0
+        for d in others:
+            eng = plans[core][cores[d]]
+            n += len(eng)
+            a = topo.addr(cores[d])
+            s = src(d)
+            regs += s[1]
+            parts.append(RemoteDMATransfer(dst_ids=[DstId(rid=a[0], pnc=a[1])], dma_engine_mask=sum(1 << e for e in eng),
+                                           remote_sem=T.sem["a_" + key], srcs=[s[0]], dsts=[dst[0]]))
+        add("G", lambda e: e.remote_dma_fused(parts, local_sem=T.sem["l_" + key]), [], regs, sem="l_" + key, inc=n, chain=False)
+
+    def recv(key, regs):
+        n = sum(len(plans[cores[q]][core]) for q in others)
+        total["a_" + key] = n
+        note({"q": "R", "tag": None, "sem": "a_" + key, "val": n, "know": {"a_" + key: n}}, regs, [])
+
+    def ghosts(name):
+        return [(name, 0, 128, V + C * q, V + C * q + C) for q in others]
+
+    def pick(bank, c0, src, s0, sel, w0, w1, tag):
+        n = 16 * (w1 - w0)
+        for b in range(16):
+            mm(X(bank, c0 + b, c0 + n, 16), X(src, s0 + b, s0 + V, 16), X(sel, w0, w1), tag=tag)
+
+    mine, LN2 = V + C * r, math.log(2.0)
+    R4, KK, QB, QH, GM, WT, NQ, CV = (col(j) for j in (4, 5, 6, 7, 8, 9, 10, 11))
+    MC, CX, CK, CJ = 16, 32, 36, 48
+    dma("Y", "bl", T.bli[:, :], rg(X("bli", 0, 24)), T.bl[:, :], [])
+    dma("S", "nb", T.nbi[:, :], rg(X("nbi", 0, 256)), T.nb[:, :], [])
+    dma("Y", "w", T.wsb[0:8, :], rg(X("wsb", 0, 4096, 1, 0, 8)), T.w[:, :], [])
+    dma("S", "x", T.xw[:, 0:V], rg(X("xw", 0, V)), T.x[:, :], [])
+    dma("Y", "xc", T.xc[:, :], rg(X("xc", 0, V)), T.x[:, :], [])
+
+    iota(X("coli", 0, 1), [[0, 1]], 0, 1, True)
+    iota(X("ir", 0, 128), [[1, 128]], 0, 0)
+    iota(X("ia", 0, 256), [[0, 64], [1, 4]], 0, 0)
+    iota(X("ic", 0, 256), [[1, 64], [0, 4]], 0, 0)
+    iota(X("jr", 0, 8), [[1, 4], [0, 2]], 4 * r, 0)
+    iota(X("jb", 0, 8), [[0, 4], [1, 2]], 0, 0)
+    iota(X("rg", 0, 128), [[1, 8], [0, 16]], 0, 0)
+    iota(X("rgam", 0, 128), [[0, 4], [1, 2], [0, 16]], 0, 0)
+    for q in range(4):
+        iota(X("aw", 32 * q, 32 * q + 32), [[16, 2], [32, 4], [1, 4]], 0, -1)
+    ts(X("coli", 1, 2), X("coli", 0, 1), 15, OP.bitwise_and)
+    cp(X("col", 0, 2), X("coli", 0, 2))
+    ts(X("col", MC, MC + 16), X("ir", 0, 16), col(1), OP.is_equal)
+    ts(X("nwa", 0, 256), X("ia", 0, 256), col(MC), OP.mult)
+    ts(X("nwb", 0, 256), X("ic", 0, 256), col(MC + 1), OP.mult)
+    tt(X("nwb", 0, 256), X("nwa", 0, 256), X("nwb", 0, 256), OP.add)
+    ts(X("jr", 0, 8), X("jr", 0, 8), col(MC + 2), OP.mult)
+    ts(X("jb", 0, 8), X("jb", 0, 8), col(MC + 3), OP.mult)
+    tt(X("col", CJ, CJ + 8), X("jr", 0, 8), X("jb", 0, 8), OP.add)
+    for j in range(8):
+        o = X("nw", 256 * j, 256 * j + 256)
+        if j % 3 == 2:
+            act(o, X("nwb", 0, 256), AF.Identity, col(CJ + j))
+        else:
+            ts(o, X("nwb", 0, 256), col(CJ + j), OP.add)
+    cp(X("bl16", 0, 24), X("bli", 0, 24))
+    cp(X("bst", 0, 384), IX("nw", V, "bl16", 0, 24))
+    send("name", lambda d: X("bst", C * d, C * d + C), X("nw", mine, mine + C))
+    act(X("nw", mine, mine + C), IX("nw", V, "bl16", 6 * r, 6 * r + 6))
+    act(X("xst", 0, 384), IX("xw", V, "bl16", 0, 24))
+    send("x", lambda d: X("xst", C * d, C * d + C), X("xw", mine, mine + C))
+    act(X("xw", mine, mine + C), IX("xw", V, "bl16", 6 * r, 6 * r + 6))
+    recv("name", ghosts("nw"))
+    recv("x", ghosts("xw"))
+
+    ts(X("ib", 0, 128), X("ir", 0, 128), col(0), OP.is_equal)
+    for d in range(2):
+        for b in range(16):
+            mm(X("pa", d * 128 + b, d * 128 + 128, 16), X("wsb", d * V + b, d * V + V, 16, 0, 8), X("ib", 0, 8, 1, 0, 8), tag="wt")
+    ts(X("e8", 0, 128, 1, 0, 8), X("rg", 0, 128, 1, 0, 8), col(0, 8), OP.is_equal)
+    cp(X("nbf", 0, 256), X("nbi", 0, 256))
+    tt(X("dn", 0, 128), X("nbf", 128, 256), X("nbf", 0, 128), OP.subtract)
+    ts(X("coli", 2, 3), X("coli", 0, 1), 4, OP.logical_shift_right)
+    cp(col(2), X("coli", 2, 3))
+    ts(X("g8", 0, 8), X("ir", 0, 8), col(2), OP.is_equal)
+    ts(col(60), col(MC), 16.0, OP.mult, col(MC + 2), OP.add)
+    ts(col(61), col(MC + 3), 64.0, OP.mult, col(MC + 1), OP.add)
+    for f in range(2):
+        ts(X("selg", 8 * f, 8 * f + 8), X("g8", 0, 8), col(60 + f), OP.mult)
+    cp(X("w0s", 0, 128), X("pa", 0, 128))
+    tt(X("bt", 0, 128), X("pa", 128, 256), X("w0s", 0, 128), OP.is_gt)
+    mm(X("pb", 0, 128), X("bt", 0, 128), X("ib", 0, 128))
+    tt(X("bd", 0, 128), X("pb", 0, 128), X("dn", 0, 128), OP.mult)
+    tt(X("hlf", 0, 128), X("nbf", 0, 128), X("bd", 0, 128), OP.add)
+    tt(X("hlf", 128, 256), X("nbf", 128, 256), X("bd", 0, 128), OP.subtract)
+    cp(X("hl16", 0, 256), X("hlf", 0, 256))
+
+    for K in range(2):
+        cp(X("gb", K * V, K * V + 1024), IX("nw", Z, "hl16", K * 128, K * 128 + 64))
+        act(X("gb", K * V + 1024, K * V + V), IX("nw", Z, "hl16", K * 128 + 64, K * 128 + 128))
+        pick("pa", K * 256, "gb", K * V, "selg", 0, 16, "gid")
+    for K in range(2):
+        for f in range(2):
+            cp(X3("snd", 0, 4, 64 * f + K * 32, 64 * f + K * 32 + 32), X("pa", K * 256 + f * 128, K * 256 + f * 128 + 128), tag="snd")
+    send("gid", lambda d: X3("snd", d, d + 1, 0, 128), X3("tg", r, r + 1, 0, 128))
+    for j in range(4):
+        mm(X("psw", 512 * j, 512 * j + 512), X("e8", 0, 128, 1, 0, 8), X("wsb", 512 * j, 512 * j + 512, 1, 0, 8))
+        act(X("w0r", 512 * j, 512 * j + 512), X("psw", 512 * j, 512 * j + 512))
+    ts(col(62), col(MC + 1), 4.0, OP.mult, col(MC), OP.add)
+    ts(col(62), col(MC + 2), 512.0, OP.mult, col(62), OP.add)
+    ts(col(62), col(MC + 3), 256.0, OP.mult, col(62), OP.add)
+    ts(X("selg", 16, 24), X("g8", 0, 8), col(62), OP.mult)
+    for K in range(2):
+        pick("pb", K * 128, "gb", K * V, "selg", 16, 24, "gid2")
+    cp(X3("tg", r, r + 1, 0, 128), X3("snd", r, r + 1, 0, 128))
+    recv("gid", [("tg", 0, 128, q * 128, q * 128 + 128) for q in others])
+    for K in range(2):
+        iota(X("ownt", 128 * K, 128 * K + 128), [[0, 8], [1, 16]], V * r, 16)
+    for q in range(4):
+        iota(X("ownp", 32 * q, 32 * q + 32), [[0, 2], [1, 4], [2048, 4]], 512 * q, 4)
+    iota(X("xw", Z, Z + 16), [[0, 16]], 0, 0)
+    iota(X("sw", Z, Z + 16), [[0, 16]], 0, 0)
+    iota(X("tw", V, V + 16), [[0, 16]], 0, 0)
+    iota(X("vl", 0, 128), [[16, 128]], V, 0)
+    iota(X("inv", 0, V), [[0, V]], V + 64, 0)
+    iota(X("id64", 0, V), [[1, V]], 64, 0)
+
+    ts(X("coli", 4, 5), X("coli", 0, 1), 3, OP.bitwise_and)
+    ts(X("coli", 5, 6), X("coli", 0, 1), 2, OP.logical_shift_right, 3, OP.bitwise_and)
+    ts(X("coli", 6, 7), X("coli", 0, 1), 5, OP.logical_shift_right, 1, OP.bitwise_and)
+    ts(X("coli", 7, 8), X("coli", 0, 1), 6, OP.logical_shift_right)
+    ts(X("coli", 8, 9), X("coli", 0, 1), 4, OP.logical_shift_right, 1, OP.bitwise_and)
+    cp(X("col", 4, 9), X("coli", 4, 9))
+    ts(CV, R4, 2.0, OP.mult, QH, OP.add)
+    act(X("wtb", 0, 1), CV, AF.Exp, 0.0, LN2)
+    ts(X("col", CX, CX + 4), X("ir", 0, 4), R4, OP.is_equal)
+    ts(X("col", CK, CK + 4), X("ir", 0, 4), KK, OP.is_equal)
+    for x in range(4):
+        ts(X("src", x * 128, x * 128 + 128), X("aw", 0, 128), float(-4 * x), OP.is_equal)
+    ts(X("i128", 0, 64), X("ib", 0, 64), 128.0, OP.mult)
+    tt(X("lst", 0, 64), X("i128", 0, 64), X("ib", 64, 128), OP.add)
+    for K in range(2):
+        ts(col(80 + K), col(CK + K), 128.0, OP.mult, col(CK + 2 + K), OP.add)
+        ts(X("sel4", 8 * K, 8 * K + 8), X("g8", 0, 8), col(80 + K), OP.mult)
+    ts(X("sel1", 0, 8), X("g8", 0, 8), col(MC), OP.mult)
+    cp(WT, X("wtb", 0, 1))
+    ts(NQ, QB, 0.0, OP.is_equal)
+    ts(X("samg", 0, 128), X("rgam", 0, 128), GM, OP.is_equal)
+    ts(X("col", 84, 88), X("col", CK, CK + 4), WT, OP.mult, NQ, OP.mult)
+    ts(X("col", 88, 92), X("col", CK, CK + 4), WT, OP.mult, QB, OP.mult)
+    for j in range(8):
+        act(X("pack", j * 128, j * 128 + 128), X("samg", 0, 128), AF.Identity, 0.0, col(84 + j))
+    ts(X("nib", 0, 128), X("ib", 0, 128), -255.0 / 512, OP.mult)
+    ts(X("iff", 0, 128), X("ir", 0, 128), col(0), OP.is_equal)
+    tt(X("rh", 0, 256), X("pb", 0, 256), X("ownt", 0, 256), OP.is_gt)
+    for K in range(2):
+        mm(X("pd", K * 128, K * 128 + 128), X("rh", K * 128, K * 128 + 128), X("ib", 0, 128))
+    cp(X("rh2", 0, 256), X("pd", 0, 256))
+
+    for q in [r] + others:
+        mm(X("pc", q * 128, q * 128 + 128), X3("tg", q, q + 1, 0, 128), X("ib", 0, 128), tag="sq")
+    cp(X("sq", 0, 512), X("pc", 0, 512))
+    for K in range(2):
+        ts(X("sti", K * 128, K * 128 + 128), X3("tg", 0, 4, K * 32, K * 32 + 32), 0.125, OP.mult, -0.4375, OP.add)
+    cp(X("stf", 0, 256), X("sti", 0, 256))
+    for q in range(4):
+        for x in range(4):
+            mm(X("psw", q * 512 + x, q * 512 + 512, 4), X("src", x * 128, x * 128 + 128), X("sq", q * 128, q * 128 + 128), tag="src")
+    for K in range(2):
+        for q in range(4):
+            mm(X("pa", K * 128, K * 128 + 128, 1, 32 * q, 32 * q + 32), X("lst", 32 * K, 32 * K + 32), X("sq", q * 128, q * 128 + 128), tag="lst")
+    for h in range(2):
+        for x in range(4):
+            o, i = X("wm", x * 2048 + h * 1024, x * 2048 + h * 1024 + 1024), X("psw", h * 1024, h * 1024 + 1024)
+            if h == 0:
+                ts(o, i, col(CX + x), OP.mult)
+            else:
+                act(o, i, AF.Identity, 0.0, col(CX + x))
+    cp(X("pl16", 0, 256), X("pa", 0, 256))
+    ts(X("blk", 0, 128), X("rg", 0, 128), col(2), OP.is_equal)
+    ts(X("tri", 0, 128), X("ir", 0, 128), col(0), OP.is_gt)
+    tt(X("lt", 0, 128), X("tri", 0, 128), X("blk", 0, 128), OP.mult)
+    ts(X("sel1f", 0, 8), X("g8", 0, 8), col(MC), OP.mult)
+
+    def places(a, b):
+        act(X("mq", a, b), X("stf", a, b), AF.Exp, 0.0, -LN2)
+        act(X("cq", a, b), X("stf", a, b), AF.Exp, 0.0, LN2)
+
+    for K in range(2):
+        cp(X("gb", K * V, K * V + 1024), IX("wm", 8192, "pl16", K * 128, K * 128 + 64))
+        act(X("gb", K * V + 1024, K * V + V), IX("wm", 8192, "pl16", K * 128 + 64, K * 128 + 128))
+        if K == 0:
+            cp(X("li", 0, 256), X("pa", 0, 256))
+            pick("pb", 0, "gb", 0, "sel4", 0, 16, "names")
+    places(0, 256)
+    tt(X("zt", 0, 128), X("pb", 0, 128), X("ownp", 0, 128), OP.is_equal)
+
+    def pack_z(before, between):
+        mm(X("pa", 0, 128), X("zt", 0, 128), X("ib", 0, 128))
+        before()
+        cp(X("zl", 0, 128), X("pa", 0, 128))
+        for h in range(2):
+            for x in range(4):
+                j = h * 4 + x
+                mm(X("psw", h * 512 + x, h * 512 + 512, 4), X("pack", j * 128, j * 128 + 128), X("zl", 0, 128), tag="pack")
+        between()
+        cp(X("ww", 0, 512), X("psw", 0, 512))
+        act(X("ww", 512, 1024), X("psw", 512, 1024))
+
+    def lists():
+        tt(X("mp", 0, 128), X("pb", 128, 256), X("ownp", 0, 128), OP.is_equal)
+        ts(X("li", 0, 256), X("li", 0, 256), 1023, OP.bitwise_and)
+        cp(X("idx", 0, 256), X("li", 0, 256))
+
+    pack_z(lambda: cp(X("pif", 0, 128), X("pb", 0, 128)), lists)
+    pick("pd", 0, "gb", V, "sel4", 0, 16, "names")
+    cp(X("mcode", 0, 128), X("zt", 0, 128))
+
+    def stage(L):
+        a = L * V
+        cp(X("gb", a, a + 1024), IX("ww", 1024, "idx", L * 128, L * 128 + 64))
+        act(X("gb", a + 1024, a + V), IX("ww", 1024, "idx", L * 128 + 64, L * 128 + 128))
+        bank, c0 = ("pc", "pd")[L // 2], (L % 2) * 128
+        mm(X(bank, c0, c0 + 128), X("nib", 0, 128), X("cq", L * 128, L * 128 + 128), True, False, tag="zz")
+        for b in range(16):
+            mm(X(bank, c0 + b, c0 + 128, 16), X("gb", a + b, a + V, 16), X("sel1", 0, 8), False, b == 15, tag="zz")
+
+    def bits(H):
+        a, bank = H * 256, ("pc", "pd")[H]
+        tt(X("yi", a, a + 256), X(bank, 0, 256), X("mq", a, a + 256), OP.mult)
+        ts(X("zi", a, a + 256), X("yi", a, a + 256), 1, OP.bitwise_and)
+
+    for t in range(2):
+        stage(0)
+        if t == 0:
+            cp(X("pif", 128, 256), X("pd", 0, 128))
+            tt(X("mlh", 0, 128), X("pd", 0, 128), X("ownp", 0, 128), OP.is_equal)
+            tt(X("mp", 128, 256), X("pd", 128, 256), X("ownp", 0, 128), OP.is_equal)
+            for K in range(2):
+                mm(X("pb", K * 128, K * 128 + 128), X("pif", K * 128, K * 128 + 128), X("iff", 0, 128))
+        stage(1)
+        if t == 0:
+            cp(X("lj", 0, 256), X("pb", 0, 256))
+            ts(X("lj", 0, 256), X("lj", 0, 256), 1023, OP.bitwise_and)
+            cp(X("idx", 256, 512), X("lj", 0, 256))
+            ts(X("sti", 256, 512), X("pif", 0, 256), 1.0 / 1024, OP.mult, -0.5 + 1.0 / 2048, OP.add)
+            cp(X("stf", 256, 512), X("sti", 256, 512))
+            places(256, 512)
+        stage(2)
+        stage(3)
+        ts(X("nz", 0, 128), X("zt", 0, 128), 0.0, OP.is_equal)
+        bits(0)
+        bits(1)
+        tt(X("pp", 0, 256), X("zi", 256, 512), X("mp", 0, 256), OP.mult)
+        tt(X("pp", 128, 256), X("pp", 128, 256), X("mlh", 0, 128), OP.max)
+        tt(X("ar", 0, 256), X("pp", 0, 256), X("zi", 0, 256), OP.is_gt)
+        tt(X("bb", 0, 128), X("ar", 128, 256), X("zi", 0, 128), OP.mult)
+        if t == 0:
+            tt(X("cd", 0, 128), X("ar", 0, 128), X("bb", 0, 128), OP.max)
+            tt(X("zt", 0, 128), X("zt", 0, 128), X("cd", 0, 128), OP.max)
+            pack_z(lambda: tt(X("cd", 0, 128), X("ar", 0, 128), X("bb", 0, 128), OP.subtract),
+                   lambda: tt(X("cd", 0, 128), X("cd", 0, 128), X("nz", 0, 128), OP.mult))
+        else:
+            tt(X("cd", 0, 128), X("ar", 0, 128), X("bb", 0, 128), OP.subtract)
+            tt(X("cd", 0, 128), X("cd", 0, 128), X("nz", 0, 128), OP.mult)
+        tt(X("mcode", 0, 128), X("mcode", 0, 128), X("cd", 0, 128), OP.add)
+    send("code", lambda d: X("mcode", 32 * d, 32 * d + 32), X("tc", 32 * r, 32 * r + 32))
+    cp(X("tc", 32 * r, 32 * r + 32), X("mcode", 32 * r, 32 * r + 32))
+    recv("code", [("tc", 0, 128, 32 * q, 32 * q + 32) for q in others])
+
+    for j in range(4):
+        mm(X("psw", 512 * j, 512 * j + 512), X("e8", 0, 128, 1, 0, 8), X("wsb", V + 512 * j, V + 512 * j + 512, 1, 0, 8))
+    for K, n in ((0, "h4"), (1, "l4")):
+        ts(X(n, 0, 128), X("hlf", K * 128, K * 128 + 128), float(Z), OP.subtract)
+        ts(X(n, 128, 256), X("rh2", K * 128, K * 128 + 128), 1.0, OP.subtract)
+    tt(X("beta", 0, 256), X("h4", 0, 256), X("l4", 0, 256), OP.add)
+    ts(X("beta", 0, 256), X("beta", 0, 256), 0.5, OP.mult)
+    tt(X("alph", 0, 256), X("h4", 0, 256), X("beta", 0, 256), OP.subtract)
+
+    for K in range(2):
+        mm(X("pc", K * 128, K * 128 + 128), X("tc", 0, 128), X("ib", 0, 128), tag="mate")
+    tt(X("t1", 0, 256), X("beta", 0, 256), X("pc", 0, 256), OP.mult)
+    tt(X("t1", 0, 256), X("t1", 0, 256), X("alph", 0, 256), OP.add)
+    tt(X("t1", 0, 256), X("t1", 0, 256), X("pc", 0, 256), OP.mult)
+    ts(X("mate", 0, 128), X("t1", 0, 128), float(Z), OP.add)
+    ts(X("rep", 0, 128), X("t1", 128, 256), 1.0, OP.add)
+    for j in range(2):
+        a, b = 1024 * j, 1024 * j + 1024
+        tt(X("xf", a, b), IX("xw", Z + 16, "mate", 64 * j, 64 * j + 64), X("xc", a, b), OP.add)
+    mm(X("pd", 0, 128), X("rep", 0, 128), X("ib", 0, 128))
+    act(X("rt", 0, 128), X("pd", 0, 128))
+    mm(X("pb", 0, 128), X("rt", 0, 128), X("tri", 0, 128))
+    act(X("up", 0, 128), X("pb", 0, 128))
+    mm(X("pd", 0, 128), X("blk", 0, 128), X("up", 0, 128), True, False, tag="num")
+    mm(X("pd", 0, 128), X("lt", 0, 128), X("rep", 0, 128), False, True, tag="num")
+    act(X("num", 0, 128), X("pd", 0, 128))
+    act(X("cn", 0, 128), X("num", 0, 128), AF.Identity, float(V * r))
+    for c in range(16):
+        act(X("sp", c, V, 16), X("cn", 0, 128), AF.Identity, 0.0, col(MC + c), tag="sp")
+    cp(X("xb", 0, 384), IX("xf", V, "bl16", 0, 24))
+    send("xs", lambda d: X("xb", C * d, C * d + C), X("xf", mine, mine + C))
+    act(X("xf", mine, mine + C), IX("xf", V, "bl16", 6 * r, 6 * r + 6))
+    recv("xs", ghosts("xf"))
+    act(X("sb", 0, 384), IX("sp", V, "bl16", 0, 24))
+    send("num", lambda d: X("sb", C * d, C * d + C), X("sp", mine, mine + C))
+    act(X("sp", mine, mine + C), IX("sp", V, "bl16", 6 * r, 6 * r + 6))
+    recv("num", ghosts("sp"))
+
+    cp(X("nb16", 0, 256), X("nbi", 0, 256))
+    ts(X("vl", 0, 128), X("vl", 0, 128), col(1), OP.add)
+    ts(X("vz", 0, 128), X("vl", 0, 128), float(V + Z), OP.subtract)
+    tt(X("off", 0, 128), X("num", 0, 128), X("vl", 0, 128), OP.subtract)
+    tt(X("off", 0, 128), X("off", 0, 128), X("rep", 0, 128), OP.mult)
+    tt(X("off", 0, 128), X("off", 0, 128), X("vl", 0, 128), OP.add)
+    cp(X("off16", 0, 128), X("off", 0, 128))
+    tt(X("ms", 0, 128), X("vz", 0, 128), X("t1", 0, 128), OP.subtract)
+    tt(X("ms", 0, 128), X("ms", 0, 128), X("rep", 0, 128), OP.mult)
+    tt(X("ms", 0, 128), X("ms", 0, 128), X("t1", 0, 128), OP.add)
+    ts(X("ms16", 0, 128), X("ms", 0, 128), float(Z), OP.add)
+
+    def invert(j):
+        o = IX("inv", 4096, "off16", 32 * j, 32 * j + 32)
+        i = X("id64", 512 * j, 512 * j + 512)
+        add("S", lambda e: e.activation(out=o[0], in_=i[0], func=AF.Silu), [("inv", 0, 128, 0, 4096)],
+            rg(i) + [("off16", 0, 128, 32 * j, 32 * j + 32)])
+
+    invert(0)
+    invert(1)
+    for j in range(4):
+        a, b = 512 * j, 512 * j + 512
+        act(X("g1", a, b), IX("xf", Z, "nb16", 128 + 32 * j, 160 + 32 * j))
+    for j in range(4):
+        a, b = 512 * j, 512 * j + 512
+        tt(X("p0", a, b), IX("xf", Z, "nb16", 32 * j, 32 * j + 32), X("w0r", a, b), OP.mult)
+    for j in range(4):
+        a, b = 512 * j, 512 * j + 512
+        tt(X("psw", a, b), X("g1", a, b), X("psw", a, b), OP.mult)
+        tt(X("sw", a, b), X("p0", a, b), X("psw", a, b), OP.add)
+    cp(X("sst", 0, 384), IX("sw", V, "bl16", 0, 24))
+    send("s", lambda d: X("sst", C * d, C * d + C), X("sw", mine, mine + C))
+    cp(X("sw", mine, mine + C), IX("sw", V, "bl16", 6 * r, 6 * r + 6))
+    recv("s", ghosts("sw"))
+    cp(X("p0", 0, V), X("sw", 0, V))
+
+    for j in range(2, 4):
+        invert(j)
+    pick("pa", 0, "inv", 0, "sel1f", 0, 8, "inv")
+    act(X("gcm", 0, V), IX("sp", Z, "ms16", 0, 128))
+    act(X("ivt", 0, 128), X("pa", 0, 128))
+    mm(X("pb", 0, 128), X("ivt", 0, 128), X("iff", 0, 128))
+    pick("pc", 0, "gcm", 0, "g8", 0, 8, "cm")
+    for j in range(2):
+        a, b = 1024 * j, 1024 * j + 1024
+        tt(X("tw", a, b), IX("sw", Z + 16, "mate", 64 * j, 64 * j + 64), X("p0", a, b), OP.add)
+    ts(X("ivi", 0, 128), X("pb", 0, 128), 64.0, OP.subtract)
+    cp(X("iv16", 0, 128), X("ivi", 0, 128))
+    for j in range(4):
+        o, i = X("yt", 512 * j, 512 * j + 512), IX("tw", V + 16, "iv16", 32 * j, 32 * j + 32)
+        if j % 2 == 0:
+            cp(o, i)
+        else:
+            act(o, i)
+        dma("Y", "y%d" % j, T.y[:, 512 * j:512 * j + 512], [], o[0], o[1])
+    act(X("cmt", 0, 128), X("pc", 0, 128))
+    mm(X("pd", 0, 128), X("cmt", 0, 128), X("iff", 0, 128))
+    act(X("cmv", 0, 128), X("pd", 0, 128))
+    dma("Y", "cm", T.cm[:, :], [], T.cmv[:, :], rg(X("cmv", 0, 128)))
+    for s, v in total.items():
+        if known["G"].get(s, 0) < v:
+            g.wait_ge(T.sem[s], v)

@@ -9,14 +9,14 @@ F32, BF, I32, U16 = "float32", "bfloat16", "int32", "uint16"
 WIDTHS = {
     F32: dict(nbf=256, col=128, jr=8, jb=8, ir=128, rg=128, rgam=128, aw=128, ownt=256, ownp=128, iff=128, g8=8, sel1f=8, vl=128,
               vz=128, w0s=128, dn=128, bd=128, hlf=256, h4=256, l4=256, beta=256, alph=256, stf=512, pif=256, t1=256, xf=2432,
-              xb=384, num=128, cn=128, off=128, ms=128, sp=2432, sb=384, g1=2048, p0=2048, sw=2448, sst=384, id64=2048, inv=4096,
-              ivt=128, gcm=2048, cmt=128, cmv=128, tw=2064, yt=2048),
-    BF: dict(wsb=4096, xw=2448, ia=256, ic=256, nwa=256, nwb=256, ib=128, nib=128, i128=64, blk=128, lt=128, tri=128, samg=128, pack=1024,
-             src=512, lst=64, selg=24, sel4=16, sel1=8, e8=128, nw=2432, bst=384, xst=384, xc=2048, wtb=2, bt=128, gb=8192, rh=256,
-             rh2=256, w0r=2048, sq=512, wm=8192, mq=512, cq=512, zt=128, zl=128, mp=256, mlh=128, ww=1024, pp=256, ar=256, bb=128,
-             nz=128, cd=128, mcode=128, tc=128, rep=128, rt=128, up=128),
-    I32: dict(bli=24, nbi=256, coli=16, li=256, sti=512, lj=256, yi=512, zi=512, ivi=128),
-    U16: dict(bl16=24, nb16=256, hl16=256, pl16=256, idx=512, mate=128, ms16=128, off16=128, iv16=128),
+              num=128, cn=128, off=128, ms=128, sp=2432, sb=384, g1=2048, p0=2048, sw=2448, sst=384, id64=2048, inv=4096,
+              ivt=128, cmt=128, cmv=128, tw=2064, xb=384, gA=384, pB=384, bq=768, bqt=256),
+    BF: dict(wsb=4096, xw=2448, ia=256, ic=256, nwa=256, nwb=256, ib=128, i128=64, blk=128, lt=128, tri=128, samg=128, pack=1024,
+             src=512, lst=64, selg=24, sel4=16, sel1=8, nw=2432, bst=384, xst=384, xc=2048, wtb=2, bt=128, gb=8192, rh=256,
+             wr=4096, sq=512, wm=8192, mq=512, zt=128, zl=128, np=256, np9=256, mlh=128, ml10=128, ww=1024, ar=256,
+             mcode=128, tc=128, rep=128, rt=128, up=128, kc=128, one=128, thr=256, tq=128),
+    I32: dict(bli=24, nbi=256, coli=16, li=256, sti=512, lj=256, yi=512, zi=512, ivi=128, bwi=48, nbw=4096, nbl=48),
+    U16: dict(bl16=24, hl16=256, pl16=256, idx=512, mate=128, ms16=128, off16=128, iv16=128, nb16=256, bw16=24, nbb16=48),
 }
 PSUM = {"psw": 2048, "pa": 512, "pb": 512, "pc": 512, "pd": 512}
 SCRATCH = {"snd": ("sbuf", [128, 4, 128], BF), "tg": ("sbuf", [128, 4, 128], BF)}
@@ -26,8 +26,9 @@ for _d in WIDTHS:
 for _n in PSUM:
     SCRATCH[_n] = ("psum", [128, PSUM[_n]], F32)
 EXCH = ["name", "x", "gid", "code", "xs", "num", "s"]
-LOADS = ["bl", "nb", "w", "x", "xc", "y0", "y1", "y2", "y3", "cm"]
+LOADS = ["bl", "nb", "w", "x", "xc", "nbw", "wr", "y0", "y1", "y2", "y3", "cm"]
 SEMAPHORES = ["cV", "cS", "cP", "cG"] + ["d_" + k for k in LOADS] + ["a_" + k for k in EXCH] + ["l_" + k for k in EXCH]
+SHARE = {"gid": (1024, 1024), "names": (1024, 512), "r0": (1024, 768, 896, 640), "r1": (1024, 1024, 896, 832), "x": 1408}
 
 
 def engine_plan(topo, src, cores):
@@ -102,8 +103,8 @@ def rank_program(g, core, T, topo):
         ap = T[name][:, i0:i1, j0:j1] if i1 - i0 > 1 else T[name][:, i0, j0:j1]
         return ap, [(name, 0, 128, i0 * 128 + j0, (i1 - 1) * 128 + j1)]
 
-    def IX(win, b, offs, c, d):
-        return T[win][:, 0:b].indirect(T[offs][:, c:d]), [(win, 0, 128, 0, b), (offs, 0, 128, c, d)]
+    def IX(win, b, offs, c, d, a=0):
+        return T[win][:, a:b].indirect(T[offs][:, c:d]), [(win, 0, 128, a, b), (offs, 0, 128, c, d)]
 
     def col(j, p1=128):
         return X("col", j, j + 1, 1, 0, p1)
@@ -144,6 +145,9 @@ def rank_program(g, core, T, topo):
             f = lambda e: e.iota(out[0], pattern, base, cm, allow_small_or_imprecise_dtypes=True)
         add("G", f, rg(out), [])
 
+    def keep(out, a):
+        add("G", lambda e: e.affine_select(out[0], a[0], [[1, 512]], OP.is_ge, 0.0, 0, 0), rg(out), rg(a))
+
     def dma(q, key, out_ap, outs, in_ap, ins):
         add(q, lambda e: e.dma_start(out=out_ap, in_=in_ap), outs, ins, sem="d_" + key, inc=16)
 
@@ -174,6 +178,10 @@ def rank_program(g, core, T, topo):
         for b in range(16):
             mm(X(bank, c0 + b, c0 + n, 16), X(src, s0 + b, s0 + V, 16), X(sel, w0, w1), tag=tag)
 
+    def share(dst, a, win, w, offs, o, n):
+        cp(X(dst, a, a + n), IX(win, w, offs, o, o + n // 16))
+        act(X(dst, a + n, a + V), IX(win, w, offs, o + n // 16, o + 128))
+
     mine, LN2 = V + C * r, math.log(2.0)
     R4, KK, QB, QH, GM, WT, NQ, CV = (col(j) for j in (4, 5, 6, 7, 8, 9, 10, 11))
     MC, CX, CK, CJ = 16, 32, 36, 48
@@ -185,135 +193,150 @@ def rank_program(g, core, T, topo):
 
     iota(X("coli", 0, 1), [[0, 1]], 0, 1, True)
     iota(X("ir", 0, 128), [[1, 128]], 0, 0)
-    iota(X("ia", 0, 256), [[0, 64], [1, 4]], 0, 0)
-    iota(X("ic", 0, 256), [[1, 64], [0, 4]], 0, 0)
     iota(X("jr", 0, 8), [[1, 4], [0, 2]], 4 * r, 0)
     iota(X("jb", 0, 8), [[0, 4], [1, 2]], 0, 0)
+    iota(X("ia", 0, 256), [[0, 64], [1, 4]], 0, 0)
+    iota(X("ic", 0, 256), [[1, 64], [0, 4]], 0, 0)
     iota(X("rg", 0, 128), [[1, 8], [0, 16]], 0, 0)
-    iota(X("rgam", 0, 128), [[0, 4], [1, 2], [0, 16]], 0, 0)
+    for q in range(4):
+        iota(X("rgam", 32 * q, 32 * q + 32), [[2, 2], [0, 8], [1, 2]], 0, 0)
     for q in range(4):
         iota(X("aw", 32 * q, 32 * q + 32), [[16, 2], [32, 4], [1, 4]], 0, -1)
     ts(X("coli", 1, 2), X("coli", 0, 1), 15, OP.bitwise_and)
-    cp(X("col", 0, 2), X("coli", 0, 2))
+    ts(X("coli", 2, 3), X("coli", 0, 1), 4, OP.logical_shift_right)
+    cp(X("col", 0, 3), X("coli", 0, 3))
     ts(X("col", MC, MC + 16), X("ir", 0, 16), col(1), OP.is_equal)
-    ts(X("nwa", 0, 256), X("ia", 0, 256), col(MC), OP.mult)
-    ts(X("nwb", 0, 256), X("ic", 0, 256), col(MC + 1), OP.mult)
-    tt(X("nwb", 0, 256), X("nwa", 0, 256), X("nwb", 0, 256), OP.add)
+    ts(X("ib", 0, 128), X("ir", 0, 128), col(0), OP.is_equal)
     ts(X("jr", 0, 8), X("jr", 0, 8), col(MC + 2), OP.mult)
     ts(X("jb", 0, 8), X("jb", 0, 8), col(MC + 3), OP.mult)
     tt(X("col", CJ, CJ + 8), X("jr", 0, 8), X("jb", 0, 8), OP.add)
+    ts(X("nwa", 0, 256), X("ia", 0, 256), col(MC), OP.mult)
+    ts(X("g8", 0, 8), X("ir", 0, 8), col(2), OP.is_equal)
+    cp(X("bl16", 0, 24), X("bli", 0, 24))
+    ts(X("nwb", 0, 256), X("ic", 0, 256), col(MC + 1), OP.mult)
+    tt(X("nwb", 0, 256), X("nwa", 0, 256), X("nwb", 0, 256), OP.add)
     for j in range(8):
         o = X("nw", 256 * j, 256 * j + 256)
-        if j % 3 == 2:
+        if j % 3 == 1:
             act(o, X("nwb", 0, 256), AF.Identity, col(CJ + j))
         else:
             ts(o, X("nwb", 0, 256), col(CJ + j), OP.add)
-    cp(X("bl16", 0, 24), X("bli", 0, 24))
     cp(X("bst", 0, 384), IX("nw", V, "bl16", 0, 24))
     send("name", lambda d: X("bst", C * d, C * d + C), X("nw", mine, mine + C))
     act(X("nw", mine, mine + C), IX("nw", V, "bl16", 6 * r, 6 * r + 6))
+
+    for d in range(2):
+        for b in range(16):
+            mm(X(("pa", "pc")[d], b, 128, 16), X("wsb", d * V + b, d * V + V, 16, 0, 8), X("ib", 0, 8, 1, 0, 8), tag="wt")
+    act(X("w0s", 0, 128), X("pa", 0, 128))
     act(X("xst", 0, 384), IX("xw", V, "bl16", 0, 24))
     send("x", lambda d: X("xst", C * d, C * d + C), X("xw", mine, mine + C))
     act(X("xw", mine, mine + C), IX("xw", V, "bl16", 6 * r, 6 * r + 6))
     recv("name", ghosts("nw"))
     recv("x", ghosts("xw"))
-
-    ts(X("ib", 0, 128), X("ir", 0, 128), col(0), OP.is_equal)
-    for d in range(2):
-        for b in range(16):
-            mm(X("pa", d * 128 + b, d * 128 + 128, 16), X("wsb", d * V + b, d * V + V, 16, 0, 8), X("ib", 0, 8, 1, 0, 8), tag="wt")
-    ts(X("e8", 0, 128, 1, 0, 8), X("rg", 0, 128, 1, 0, 8), col(0, 8), OP.is_equal)
     cp(X("nbf", 0, 256), X("nbi", 0, 256))
     tt(X("dn", 0, 128), X("nbf", 128, 256), X("nbf", 0, 128), OP.subtract)
-    ts(X("coli", 2, 3), X("coli", 0, 1), 4, OP.logical_shift_right)
-    cp(col(2), X("coli", 2, 3))
-    ts(X("g8", 0, 8), X("ir", 0, 8), col(2), OP.is_equal)
+    tt(X("bt", 0, 128), X("pc", 0, 128), X("w0s", 0, 128), OP.is_gt)
+    mm(X("pb", 0, 128), X("bt", 0, 128), X("ib", 0, 128))
     ts(col(60), col(MC), 16.0, OP.mult, col(MC + 2), OP.add)
     ts(col(61), col(MC + 3), 64.0, OP.mult, col(MC + 1), OP.add)
-    for f in range(2):
-        ts(X("selg", 8 * f, 8 * f + 8), X("g8", 0, 8), col(60 + f), OP.mult)
-    cp(X("w0s", 0, 128), X("pa", 0, 128))
-    tt(X("bt", 0, 128), X("pa", 128, 256), X("w0s", 0, 128), OP.is_gt)
-    mm(X("pb", 0, 128), X("bt", 0, 128), X("ib", 0, 128))
     tt(X("bd", 0, 128), X("pb", 0, 128), X("dn", 0, 128), OP.mult)
     tt(X("hlf", 0, 128), X("nbf", 0, 128), X("bd", 0, 128), OP.add)
+    cp(X("hl16", 0, 128), X("hlf", 0, 128))
     tt(X("hlf", 128, 256), X("nbf", 128, 256), X("bd", 0, 128), OP.subtract)
-    cp(X("hl16", 0, 256), X("hlf", 0, 256))
-
-    for K in range(2):
-        cp(X("gb", K * V, K * V + 1024), IX("nw", Z, "hl16", K * 128, K * 128 + 64))
-        act(X("gb", K * V + 1024, K * V + V), IX("nw", Z, "hl16", K * 128 + 64, K * 128 + 128))
-        pick("pa", K * 256, "gb", K * V, "selg", 0, 16, "gid")
-    for K in range(2):
-        for f in range(2):
-            cp(X3("snd", 0, 4, 64 * f + K * 32, 64 * f + K * 32 + 32), X("pa", K * 256 + f * 128, K * 256 + f * 128 + 128), tag="snd")
-    send("gid", lambda d: X3("snd", d, d + 1, 0, 128), X3("tg", r, r + 1, 0, 128))
-    for j in range(4):
-        mm(X("psw", 512 * j, 512 * j + 512), X("e8", 0, 128, 1, 0, 8), X("wsb", 512 * j, 512 * j + 512, 1, 0, 8))
-        act(X("w0r", 512 * j, 512 * j + 512), X("psw", 512 * j, 512 * j + 512))
+    cp(X("hl16", 128, 256), X("hlf", 128, 256))
+    for f in range(2):
+        ts(X("selg", 8 * f, 8 * f + 8), X("g8", 0, 8), col(60 + f), OP.mult)
     ts(col(62), col(MC + 1), 4.0, OP.mult, col(MC), OP.add)
     ts(col(62), col(MC + 2), 512.0, OP.mult, col(62), OP.add)
     ts(col(62), col(MC + 3), 256.0, OP.mult, col(62), OP.add)
     ts(X("selg", 16, 24), X("g8", 0, 8), col(62), OP.mult)
+    ts(X("coli", 3, 4), X("coli", 0, 1), 1, OP.logical_shift_right, 1, OP.bitwise_and)
+    ts(X("coli", 4, 5), X("coli", 0, 1), 3, OP.bitwise_and)
+    ts(X("coli", 5, 6), X("coli", 0, 1), 2, OP.logical_shift_right, 3, OP.bitwise_and)
+    ts(X("coli", 6, 7), X("coli", 0, 1), 5, OP.logical_shift_right, 1, OP.bitwise_and)
+    ts(X("coli", 7, 8), X("coli", 0, 1), 6, OP.logical_shift_right)
+    ts(X("coli", 8, 9), X("coli", 0, 1), 4, OP.logical_shift_right, 1, OP.bitwise_and)
+    cp(X("col", 3, 9), X("coli", 3, 9))
+    ts(CV, R4, 2.0, OP.mult, QH, OP.add)
+    ts(X("col", CX, CX + 4), X("ir", 0, 4), R4, OP.is_equal)
+    ts(X("col", CK, CK + 4), X("ir", 0, 4), KK, OP.is_equal)
+
     for K in range(2):
-        pick("pb", K * 128, "gb", K * V, "selg", 16, 24, "gid2")
+        share("gb", K * V, "nw", Z, "hl16", K * 128, SHARE["gid"][K])
+        pick("pa", K * 256, "gb", K * V, "selg", 0, 16, "gid")
+    for K in range(2):
+        for f in range(2):
+            cp(X3("snd", 0, 4, 64 * f + K * 32, 64 * f + K * 32 + 32), X("pa", K * 256 + f * 128, K * 256 + f * 128 + 128), tag="snd")
+    act(X("wtb", 0, 1), CV, AF.Exp, 0.0, 2 * LN2)
+    send("gid", lambda d: X3("snd", d, d + 1, 0, 128), X3("tg", r, r + 1, 0, 128))
+    for K in range(2):
+        pick("pb", 256 + K * 128, "gb", K * V, "selg", 16, 24, "gid2")
     cp(X3("tg", r, r + 1, 0, 128), X3("snd", r, r + 1, 0, 128))
     recv("gid", [("tg", 0, 128, q * 128, q * 128 + 128) for q in others])
     for K in range(2):
         iota(X("ownt", 128 * K, 128 * K + 128), [[0, 8], [1, 16]], V * r, 16)
     for q in range(4):
         iota(X("ownp", 32 * q, 32 * q + 32), [[0, 2], [1, 4], [2048, 4]], 512 * q, 4)
+    iota(X("kc", 0, 128), [[0, 128]], 8192, 0)
+    iota(X("one", 0, 128), [[0, 128]], 1, 0)
     iota(X("xw", Z, Z + 16), [[0, 16]], 0, 0)
     iota(X("sw", Z, Z + 16), [[0, 16]], 0, 0)
     iota(X("tw", V, V + 16), [[0, 16]], 0, 0)
     iota(X("vl", 0, 128), [[16, 128]], V, 0)
+    iota(X("nbw", 0, 4096), [[0, 4096]], 0, 0, True)
     iota(X("inv", 0, V), [[0, V]], V + 64, 0)
     iota(X("id64", 0, V), [[1, V]], 64, 0)
+    for c in range(16):
+        dma("Y", "wr", T.wr[c:128:16, :], [("wr", 16 * k + c, 16 * k + c + 1, 0, 4096) for k in range(8)], T.w[:, :],
+            [("tg", 0, 128, 0, 512)])
+    for k in range(8):
+        dma("Y", "nbw", T.nbw[16 * k:16 * k + 1, :], [("nbw", 16 * k, 16 * k + 1, 0, 4096)], T.nb[16 * k:16 * k + 16, :], [])
 
-    ts(X("coli", 4, 5), X("coli", 0, 1), 3, OP.bitwise_and)
-    ts(X("coli", 5, 6), X("coli", 0, 1), 2, OP.logical_shift_right, 3, OP.bitwise_and)
-    ts(X("coli", 6, 7), X("coli", 0, 1), 5, OP.logical_shift_right, 1, OP.bitwise_and)
-    ts(X("coli", 7, 8), X("coli", 0, 1), 6, OP.logical_shift_right)
-    ts(X("coli", 8, 9), X("coli", 0, 1), 4, OP.logical_shift_right, 1, OP.bitwise_and)
-    cp(X("col", 4, 9), X("coli", 4, 9))
-    ts(CV, R4, 2.0, OP.mult, QH, OP.add)
-    act(X("wtb", 0, 1), CV, AF.Exp, 0.0, LN2)
-    ts(X("col", CX, CX + 4), X("ir", 0, 4), R4, OP.is_equal)
-    ts(X("col", CK, CK + 4), X("ir", 0, 4), KK, OP.is_equal)
     for x in range(4):
         ts(X("src", x * 128, x * 128 + 128), X("aw", 0, 128), float(-4 * x), OP.is_equal)
-    ts(X("i128", 0, 64), X("ib", 0, 64), 128.0, OP.mult)
+    act(X("i128", 0, 64), X("ib", 0, 64), AF.Identity, 0.0, 128.0)
     tt(X("lst", 0, 64), X("i128", 0, 64), X("ib", 64, 128), OP.add)
     for K in range(2):
         ts(col(80 + K), col(CK + K), 128.0, OP.mult, col(CK + 2 + K), OP.add)
         ts(X("sel4", 8 * K, 8 * K + 8), X("g8", 0, 8), col(80 + K), OP.mult)
-    ts(X("sel1", 0, 8), X("g8", 0, 8), col(MC), OP.mult)
+    tt(col(63), col(MC), col(MC + 1), OP.add)
+    ts(X("sel1", 0, 8), X("g8", 0, 8), col(63), OP.mult)
     cp(WT, X("wtb", 0, 1))
     ts(NQ, QB, 0.0, OP.is_equal)
-    ts(X("samg", 0, 128), X("rgam", 0, 128), GM, OP.is_equal)
+    ts(col(64), GM, 2.0, OP.mult, col(3), OP.add)
+    ts(X("iff", 0, 128), X("ir", 0, 128), col(0), OP.is_equal)
+    ts(X("samg", 0, 128), X("rgam", 0, 128), col(64), OP.is_equal)
     ts(X("col", 84, 88), X("col", CK, CK + 4), WT, OP.mult, NQ, OP.mult)
     ts(X("col", 88, 92), X("col", CK, CK + 4), WT, OP.mult, QB, OP.mult)
     for j in range(8):
         act(X("pack", j * 128, j * 128 + 128), X("samg", 0, 128), AF.Identity, 0.0, col(84 + j))
-    ts(X("nib", 0, 128), X("ib", 0, 128), -255.0 / 512, OP.mult)
-    ts(X("iff", 0, 128), X("ir", 0, 128), col(0), OP.is_equal)
-    tt(X("rh", 0, 256), X("pb", 0, 256), X("ownt", 0, 256), OP.is_gt)
+    tt(X("rh", 0, 256), X("pb", 256, 512), X("ownt", 0, 256), OP.is_gt)
     for K in range(2):
         mm(X("pd", K * 128, K * 128 + 128), X("rh", K * 128, K * 128 + 128), X("ib", 0, 128))
-    cp(X("rh2", 0, 256), X("pd", 0, 256))
+    for K, n in ((0, "h4"), (1, "l4")):
+        act(X(n, 0, 128), X("hlf", K * 128, K * 128 + 128), AF.Identity, -float(Z))
+        act(X(n, 128, 256), X("pd", K * 128, K * 128 + 128), AF.Identity, -1.0)
 
     for q in [r] + others:
         mm(X("pc", q * 128, q * 128 + 128), X3("tg", q, q + 1, 0, 128), X("ib", 0, 128), tag="sq")
     cp(X("sq", 0, 512), X("pc", 0, 512))
-    for K in range(2):
-        ts(X("sti", K * 128, K * 128 + 128), X3("tg", 0, 4, K * 32, K * 32 + 32), 0.125, OP.mult, -0.4375, OP.add)
-    cp(X("stf", 0, 256), X("sti", 0, 256))
     for q in range(4):
         for x in range(4):
             mm(X("psw", q * 512 + x, q * 512 + 512, 4), X("src", x * 128, x * 128 + 128), X("sq", q * 128, q * 128 + 128), tag="src")
     for K in range(2):
         for q in range(4):
             mm(X("pa", K * 128, K * 128 + 128, 1, 32 * q, 32 * q + 32), X("lst", 32 * K, 32 * K + 32), X("sq", q * 128, q * 128 + 128), tag="lst")
+    cp(X("nb16", 0, 256), X("nbi", 0, 256))
+    ts(X("blk", 0, 128), X("rg", 0, 128), col(2), OP.is_equal)
+    ts(X("tri", 0, 128), X("ir", 0, 128), col(0), OP.is_gt)
+    tt(X("lt", 0, 128), X("tri", 0, 128), X("blk", 0, 128), OP.mult)
+    ts(X("sel1f", 0, 8), X("g8", 0, 8), col(MC), OP.mult)
+    ts(X("bwi", 0, 24), X("bli", 0, 24), 4, OP.logical_shift_right)
+    ts(X("bwi", 24, 48), X("bli", 0, 24), 15, OP.bitwise_and)
+    ts(X("bwi", 24, 48), X("bwi", 24, 48), 256.0, OP.mult)
+    tt(X("bwi", 0, 24), X("bwi", 0, 24), X("bwi", 24, 48), OP.add)
+    cp(X("bw16", 0, 24), X("bwi", 0, 24))
     for h in range(2):
         for x in range(4):
             o, i = X("wm", x * 2048 + h * 1024, x * 2048 + h * 1024 + 1024), X("psw", h * 1024, h * 1024 + 1024)
@@ -322,26 +345,26 @@ def rank_program(g, core, T, topo):
             else:
                 act(o, i, AF.Identity, 0.0, col(CX + x))
     cp(X("pl16", 0, 256), X("pa", 0, 256))
-    ts(X("blk", 0, 128), X("rg", 0, 128), col(2), OP.is_equal)
-    ts(X("tri", 0, 128), X("ir", 0, 128), col(0), OP.is_gt)
-    tt(X("lt", 0, 128), X("tri", 0, 128), X("blk", 0, 128), OP.mult)
-    ts(X("sel1f", 0, 8), X("g8", 0, 8), col(MC), OP.mult)
 
     def places(a, b):
-        act(X("mq", a, b), X("stf", a, b), AF.Exp, 0.0, -LN2)
-        act(X("cq", a, b), X("stf", a, b), AF.Exp, 0.0, LN2)
+        act(X("mq", a, b), X("stf", a, b), AF.Exp, 0.0, -2 * LN2)
 
     for K in range(2):
-        cp(X("gb", K * V, K * V + 1024), IX("wm", 8192, "pl16", K * 128, K * 128 + 64))
-        act(X("gb", K * V + 1024, K * V + V), IX("wm", 8192, "pl16", K * 128 + 64, K * 128 + 128))
+        share("gb", K * V, "wm", 8192, "pl16", K * 128, SHARE["names"][K])
         if K == 0:
             cp(X("li", 0, 256), X("pa", 0, 256))
+            for k in range(2):
+                ts(X("sti", k * 128, k * 128 + 128), X3("tg", 0, 4, k * 32, k * 32 + 32), 0.125, OP.mult, -0.4375, OP.add)
+            cp(X("stf", 0, 256), X("sti", 0, 256))
             pick("pb", 0, "gb", 0, "sel4", 0, 16, "names")
     places(0, 256)
+    act(X("vl", 0, 128), X("vl", 0, 128), AF.Identity, col(1))
+    act(X("vz", 0, 128), X("vl", 0, 128), AF.Identity, -float(V + Z))
     tt(X("zt", 0, 128), X("pb", 0, 128), X("ownp", 0, 128), OP.is_equal)
 
-    def pack_z(before, between):
-        mm(X("pa", 0, 128), X("zt", 0, 128), X("ib", 0, 128))
+    def pack_z(parts, before, between):
+        for i, p in enumerate(parts):
+            mm(X("pa", 0, 128), p, X("ib", 0, 128), i == 0, i == len(parts) - 1, tag="zl")
         before()
         cp(X("zl", 0, 128), X("pa", 0, 128))
         for h in range(2):
@@ -353,115 +376,155 @@ def rank_program(g, core, T, topo):
         act(X("ww", 512, 1024), X("psw", 512, 1024))
 
     def lists():
-        tt(X("mp", 0, 128), X("pb", 128, 256), X("ownp", 0, 128), OP.is_equal)
+        tt(X("np", 0, 128), X("pb", 128, 256), X("ownp", 0, 128), OP.not_equal)
         ts(X("li", 0, 256), X("li", 0, 256), 1023, OP.bitwise_and)
         cp(X("idx", 0, 256), X("li", 0, 256))
 
-    pack_z(lambda: cp(X("pif", 0, 128), X("pb", 0, 128)), lists)
+    pack_z([X("zt", 0, 128)], lambda: cp(X("pif", 0, 128), X("pb", 0, 128)), lists)
     pick("pd", 0, "gb", V, "sel4", 0, 16, "names")
     cp(X("mcode", 0, 128), X("zt", 0, 128))
 
-    def stage(L):
-        a = L * V
-        cp(X("gb", a, a + 1024), IX("ww", 1024, "idx", L * 128, L * 128 + 64))
-        act(X("gb", a + 1024, a + V), IX("ww", 1024, "idx", L * 128 + 64, L * 128 + 128))
+    def ask(L, n):
+        share("gb", L * V, "ww", 1024, "idx", L * 128, n)
+
+    def answer(L):
         bank, c0 = ("pc", "pd")[L // 2], (L % 2) * 128
-        mm(X(bank, c0, c0 + 128), X("nib", 0, 128), X("cq", L * 128, L * 128 + 128), True, False, tag="zz")
+        if L == 3:
+            mm(X(bank, c0, c0 + 128), X("kc", 0, 128), X("one", 0, 128), True, False, tag="zz")
         for b in range(16):
-            mm(X(bank, c0 + b, c0 + 128, 16), X("gb", a + b, a + V, 16), X("sel1", 0, 8), False, b == 15, tag="zz")
+            mm(X(bank, c0 + b, c0 + 128, 16), X("gb", L * V + b, L * V + V, 16), X("sel1", 0, 8), L != 3, L != 3 or b == 15, tag="zz")
 
     def bits(H):
         a, bank = H * 256, ("pc", "pd")[H]
         tt(X("yi", a, a + 256), X(bank, 0, 256), X("mq", a, a + 256), OP.mult)
         ts(X("zi", a, a + 256), X("yi", a, a + 256), 1, OP.bitwise_and)
 
+    def border_lists(d):
+        for b in range(16):
+            mm(X("pa", d * 128 + b, d * 128 + 128, 16, 0, 24), X("bq", d * 384 + b, d * 384 + 384, 16), X("sel1f", 0, 8), tag="bq")
+
+    ARH, ARL = X("ar", 0, 128), X("ar", 128, 256)
     for t in range(2):
-        stage(0)
+        n = SHARE["r%d" % t]
+        if t == 1:
+            border_lists(0)
+        ask(0, n[0])
         if t == 0:
             cp(X("pif", 128, 256), X("pd", 0, 128))
-            tt(X("mlh", 0, 128), X("pd", 0, 128), X("ownp", 0, 128), OP.is_equal)
-            tt(X("mp", 128, 256), X("pd", 128, 256), X("ownp", 0, 128), OP.is_equal)
             for K in range(2):
                 mm(X("pb", K * 128, K * 128 + 128), X("pif", K * 128, K * 128 + 128), X("iff", 0, 128))
-        stage(1)
+            tt(X("np", 128, 256), X("pd", 128, 256), X("ownp", 0, 128), OP.not_equal)
+            tt(X("mlh", 0, 128), X("pd", 0, 128), X("ownp", 0, 128), OP.is_equal)
+        answer(0)
+        ask(1, n[1])
         if t == 0:
             cp(X("lj", 0, 256), X("pb", 0, 256))
             ts(X("lj", 0, 256), X("lj", 0, 256), 1023, OP.bitwise_and)
             cp(X("idx", 256, 512), X("lj", 0, 256))
+            act(X("np9", 0, 256), X("np", 0, 256), AF.Identity, 0.0, 9.0)
+            act(X("ml10", 0, 128), X("mlh", 0, 128), AF.Identity, 0.0, 10.0)
             ts(X("sti", 256, 512), X("pif", 0, 256), 1.0 / 1024, OP.mult, -0.5 + 1.0 / 2048, OP.add)
-            cp(X("stf", 256, 512), X("sti", 256, 512))
-            places(256, 512)
-        stage(2)
-        stage(3)
-        ts(X("nz", 0, 128), X("zt", 0, 128), 0.0, OP.is_equal)
-        bits(0)
-        bits(1)
-        tt(X("pp", 0, 256), X("zi", 256, 512), X("mp", 0, 256), OP.mult)
-        tt(X("pp", 128, 256), X("pp", 128, 256), X("mlh", 0, 128), OP.max)
-        tt(X("ar", 0, 256), X("pp", 0, 256), X("zi", 0, 256), OP.is_gt)
-        tt(X("bb", 0, 128), X("ar", 128, 256), X("zi", 0, 128), OP.mult)
+        answer(1)
         if t == 0:
-            tt(X("cd", 0, 128), X("ar", 0, 128), X("bb", 0, 128), OP.max)
-            tt(X("zt", 0, 128), X("zt", 0, 128), X("cd", 0, 128), OP.max)
-            pack_z(lambda: tt(X("cd", 0, 128), X("ar", 0, 128), X("bb", 0, 128), OP.subtract),
-                   lambda: tt(X("cd", 0, 128), X("cd", 0, 128), X("nz", 0, 128), OP.mult))
-        else:
-            tt(X("cd", 0, 128), X("ar", 0, 128), X("bb", 0, 128), OP.subtract)
-            tt(X("cd", 0, 128), X("cd", 0, 128), X("nz", 0, 128), OP.mult)
-        tt(X("mcode", 0, 128), X("mcode", 0, 128), X("cd", 0, 128), OP.add)
+            tt(X("stf", 256, 512), X("sti", 256, 512), X("np9", 0, 256), OP.max)
+            tt(X("stf", 384, 512), X("stf", 384, 512), X("ml10", 0, 128), OP.max)
+        ask(2, n[2])
+        answer(2)
+        if t == 0:
+            places(256, 512)
+        ask(3, n[3])
+        answer(3)
+        bits(0)
+        tt(X("tq", 0, 128), X("zi", 0, 128), X("zt", 0, 128), OP.is_le)
+        tt(X("thr", 0, 128), X("zi", 0, 128), X("zt", 0, 128), OP.max)
+        tt(X("thr", 128, 256), X("zi", 128, 256), X("tq", 0, 128), OP.max)
+        cp(X("bq", 384 * t, 384 * t + 384), IX("nbw", 4096, "bw16", 0, 24, 128 * t))
+        bits(1)
+        tt(X("ar", 0, 256), X("zi", 256, 512), X("thr", 0, 256), OP.is_gt)
+        if t == 0:
+            def more():
+                tt(X("zt", 0, 128), X("zt", 0, 128), ARH, OP.add)
+                tt(X("zt", 0, 128), X("zt", 0, 128), ARL, OP.add)
+            pack_z([X("zt", 0, 128), ARH, ARL], lambda: None, more)
+        tt(X("mcode", 0, 128), X("mcode", 0, 128), ARH, OP.add)
+        tt(X("mcode", 0, 128), X("mcode", 0, 128), ARL, OP.subtract)
+    border_lists(1)
+    act(X("bqt", 0, 256, 1, 0, 24), X("pa", 0, 256, 1, 0, 24), AF.Silu, 64.0)
     send("code", lambda d: X("mcode", 32 * d, 32 * d + 32), X("tc", 32 * r, 32 * r + 32))
     cp(X("tc", 32 * r, 32 * r + 32), X("mcode", 32 * r, 32 * r + 32))
     recv("code", [("tc", 0, 128, 32 * q, 32 * q + 32) for q in others])
 
-    for j in range(4):
-        mm(X("psw", 512 * j, 512 * j + 512), X("e8", 0, 128, 1, 0, 8), X("wsb", V + 512 * j, V + 512 * j + 512, 1, 0, 8))
-    for K, n in ((0, "h4"), (1, "l4")):
-        ts(X(n, 0, 128), X("hlf", K * 128, K * 128 + 128), float(Z), OP.subtract)
-        ts(X(n, 128, 256), X("rh2", K * 128, K * 128 + 128), 1.0, OP.subtract)
     tt(X("beta", 0, 256), X("h4", 0, 256), X("l4", 0, 256), OP.add)
     ts(X("beta", 0, 256), X("beta", 0, 256), 0.5, OP.mult)
     tt(X("alph", 0, 256), X("h4", 0, 256), X("beta", 0, 256), OP.subtract)
+    for d in range(2):
+        act(X("gb", V + 384 * d, V + 384 * d + 384), IX("wr", V + V * d, "bl16", 0, 24, V * d))
+    for d in range(2):
+        mm(X("pc", 256 + 24 * d, 280 + 24 * d), X("bqt", d * 128, d * 128 + 128, 1, 0, 24), X("iff", 0, 24, 1, 0, 24))
 
-    for K in range(2):
-        mm(X("pc", K * 128, K * 128 + 128), X("tc", 0, 128), X("ib", 0, 128), tag="mate")
-    tt(X("t1", 0, 256), X("beta", 0, 256), X("pc", 0, 256), OP.mult)
-    tt(X("t1", 0, 256), X("t1", 0, 256), X("alph", 0, 256), OP.add)
-    tt(X("t1", 0, 256), X("t1", 0, 256), X("pc", 0, 256), OP.mult)
+    mm(X("pc", 0, 128), X("tc", 0, 128), X("ib", 0, 128))
+
+    def quad(a):
+        tt(X("t1", a, a + 128), X("beta", a, a + 128), X("pc", 0, 128), OP.mult)
+        tt(X("t1", a, a + 128), X("t1", a, a + 128), X("alph", a, a + 128), OP.add)
+        tt(X("t1", a, a + 128), X("t1", a, a + 128), X("pc", 0, 128), OP.mult)
+
+    for j in range(4):
+        mm(X("psw", 512 * j, 512 * j + 512), X("ib", 0, 128), X("wr", V + 512 * j, V + 512 * j + 512))
+    quad(0)
     ts(X("mate", 0, 128), X("t1", 0, 128), float(Z), OP.add)
-    ts(X("rep", 0, 128), X("t1", 128, 256), 1.0, OP.add)
-    for j in range(2):
-        a, b = 1024 * j, 1024 * j + 1024
-        tt(X("xf", a, b), IX("xw", Z + 16, "mate", 64 * j, 64 * j + 64), X("xc", a, b), OP.add)
-    mm(X("pd", 0, 128), X("rep", 0, 128), X("ib", 0, 128))
-    act(X("rt", 0, 128), X("pd", 0, 128))
-    mm(X("pb", 0, 128), X("rt", 0, 128), X("tri", 0, 128))
-    act(X("up", 0, 128), X("pb", 0, 128))
-    mm(X("pd", 0, 128), X("blk", 0, 128), X("up", 0, 128), True, False, tag="num")
-    mm(X("pd", 0, 128), X("lt", 0, 128), X("rep", 0, 128), False, True, tag="num")
-    act(X("num", 0, 128), X("pd", 0, 128))
-    act(X("cn", 0, 128), X("num", 0, 128), AF.Identity, float(V * r))
-    for c in range(16):
-        act(X("sp", c, V, 16), X("cn", 0, 128), AF.Identity, 0.0, col(MC + c), tag="sp")
-    cp(X("xb", 0, 384), IX("xf", V, "bl16", 0, 24))
+    nx = SHARE["x"]
+    tt(X("xf", 0, nx), IX("xw", Z + 16, "mate", 0, nx // 16), X("xc", 0, nx), OP.add)
+    for i, (bank, a, b) in enumerate((("pa", nx, nx + 512), ("pb", nx + 512, V))):
+        act(X("gb", a - nx, b - nx), IX("xw", Z + 16, "mate", a // 16, b // 16))
+        mm(X(bank, 0, b - a), X("ib", 0, 128), X("xc", a, b), True, False, tag="gx")
+        mm(X(bank, 0, b - a), X("ib", 0, 128), X("gb", a - nx, b - nx), False, True, tag="gx")
+    for bank, a, b in (("pa", nx, nx + 512), ("pb", nx + 512, V)):
+        act(X("xf", a, b), X(bank, 0, b - a))
+    mm(X("pb", 0, 384), X("ib", 0, 128), X("gb", V + 384, V + 768))
+    cp(X("xb", 0, 192), IX("xf", V, "bl16", 0, 12))
+    act(X("xb", 192, 384), IX("xf", V, "bl16", 12, 24))
     send("xs", lambda d: X("xb", C * d, C * d + C), X("xf", mine, mine + C))
-    act(X("xf", mine, mine + C), IX("xf", V, "bl16", 6 * r, 6 * r + 6))
+    act(X("xf", mine, mine + C), X("xb", C * r, C * r + C))
     recv("xs", ghosts("xf"))
-    act(X("sb", 0, 384), IX("sp", V, "bl16", 0, 24))
-    send("num", lambda d: X("sb", C * d, C * d + C), X("sp", mine, mine + C))
-    act(X("sp", mine, mine + C), IX("sp", V, "bl16", 6 * r, 6 * r + 6))
-    recv("num", ghosts("sp"))
 
-    cp(X("nb16", 0, 256), X("nbi", 0, 256))
-    ts(X("vl", 0, 128), X("vl", 0, 128), col(1), OP.add)
-    ts(X("vz", 0, 128), X("vl", 0, 128), float(V + Z), OP.subtract)
-    tt(X("off", 0, 128), X("num", 0, 128), X("vl", 0, 128), OP.subtract)
-    tt(X("off", 0, 128), X("off", 0, 128), X("rep", 0, 128), OP.mult)
-    tt(X("off", 0, 128), X("off", 0, 128), X("vl", 0, 128), OP.add)
-    cp(X("off16", 0, 128), X("off", 0, 128))
+    quad(128)
+    ts(X("rep", 0, 128), X("t1", 128, 256), 1.0, OP.add)
+    mm(X("pd", 0, 128), X("rep", 0, 128), X("ib", 0, 128))
+    ts(X("nbl", 0, 48), X("pc", 256, 304), 64.0, OP.subtract)
+    cp(X("nbb16", 0, 48), X("nbl", 0, 48))
     tt(X("ms", 0, 128), X("vz", 0, 128), X("t1", 0, 128), OP.subtract)
     tt(X("ms", 0, 128), X("ms", 0, 128), X("rep", 0, 128), OP.mult)
     tt(X("ms", 0, 128), X("ms", 0, 128), X("t1", 0, 128), OP.add)
     ts(X("ms16", 0, 128), X("ms", 0, 128), float(Z), OP.add)
+    act(X("rt", 0, 128), X("pd", 0, 128))
+    mm(X("pd", 128, 256), X("rt", 0, 128), X("tri", 0, 128))
+    act(X("up", 0, 128), X("pd", 128, 256))
+    mm(X("pd", 0, 128), X("blk", 0, 128), X("up", 0, 128), True, False, tag="num")
+    mm(X("pd", 0, 128), X("lt", 0, 128), X("rep", 0, 128), False, True, tag="num")
+    act(X("num", 0, 128), X("pd", 0, 128))
+    act(X("cn", 0, 128), X("pd", 0, 128), AF.Identity, float(V * r))
+    tt(X("off", 0, 128), X("num", 0, 128), X("vl", 0, 128), OP.subtract)
+    tt(X("off", 0, 128), X("off", 0, 128), X("rep", 0, 128), OP.mult)
+    tt(X("off", 0, 128), X("off", 0, 128), X("vl", 0, 128), OP.add)
+    cp(X("off16", 0, 128), X("off", 0, 128))
+
+    def SP(c):
+        return X("sp", c, V, 16)[0], [("sp%d" % c, 0, 128, 0, 128)]
+
+    def numbers(offs, c, d, b):
+        ap, regs = IX("sp", b, offs, c, d)
+        return ap, regs + [y for k in range(16) for y in SP(k)[1]]
+
+    for c in range(16):
+        if c < 4:
+            ts(SP(c), X("cn", 0, 128), col(MC + c), OP.mult)
+        else:
+            act(SP(c), X("cn", 0, 128), AF.Identity, 0.0, col(MC + c))
+    act(X("sb", 0, 384), numbers("bl16", 0, 24, V))
+    send("num", lambda d: X("sb", C * d, C * d + C), X("sp", mine, mine + C))
+    act(X("sp", mine, mine + C), X("sb", C * r, C * r + C))
+    recv("num", ghosts("sp"))
 
     def invert(j):
         o = IX("inv", 4096, "off16", 32 * j, 32 * j + 32)
@@ -469,43 +532,48 @@ def rank_program(g, core, T, topo):
         add("S", lambda e: e.activation(out=o[0], in_=i[0], func=AF.Silu), [("inv", 0, 128, 0, 4096)],
             rg(i) + [("off16", 0, 128, 32 * j, 32 * j + 32)])
 
-    invert(0)
-    invert(1)
+    def times_w0(a, b):
+        tt(X("p0", a, b), IX("xf", Z, "nb16", a // 16, b // 16), X("wr", a, b), OP.mult)
+
+    act(X("gA", 0, 384), IX("xf", Z, "nbb16", 24, 48))
+    tt(X("pB", 0, 384), IX("xf", Z, "nbb16", 0, 24), X("gb", V, V + 384), OP.mult)
+    times_w0(0, 512)
+    tt(X("pb", 0, 384), X("gA", 0, 384), X("pb", 0, 384), OP.mult)
+    tt(X("sst", 0, 384), X("pB", 0, 384), X("pb", 0, 384), OP.add)
+    send("s", lambda d: X("sst", C * d, C * d + C), X("sw", mine, mine + C))
+    recv("s", ghosts("sw"))
+
     for j in range(4):
         a, b = 512 * j, 512 * j + 512
         act(X("g1", a, b), IX("xf", Z, "nb16", 128 + 32 * j, 160 + 32 * j))
+        if j > 0:
+            invert(j - 1)
+    invert(3)
+    act(X("sw", mine, mine + C), X("sst", C * r, C * r + C))
     for j in range(4):
         a, b = 512 * j, 512 * j + 512
-        tt(X("p0", a, b), IX("xf", Z, "nb16", 32 * j, 32 * j + 32), X("w0r", a, b), OP.mult)
-    for j in range(4):
-        a, b = 512 * j, 512 * j + 512
+        if j > 0:
+            times_w0(a, b)
         tt(X("psw", a, b), X("g1", a, b), X("psw", a, b), OP.mult)
         tt(X("sw", a, b), X("p0", a, b), X("psw", a, b), OP.add)
-    cp(X("sst", 0, 384), IX("sw", V, "bl16", 0, 24))
-    send("s", lambda d: X("sst", C * d, C * d + C), X("sw", mine, mine + C))
-    cp(X("sw", mine, mine + C), IX("sw", V, "bl16", 6 * r, 6 * r + 6))
-    recv("s", ghosts("sw"))
-    cp(X("p0", 0, V), X("sw", 0, V))
-
-    for j in range(2, 4):
-        invert(j)
+        keep(X("p0", a, b), X("sw", a, b))
     pick("pa", 0, "inv", 0, "sel1f", 0, 8, "inv")
-    act(X("gcm", 0, V), IX("sp", Z, "ms16", 0, 128))
+    act(X("g1", 0, V), numbers("ms16", 0, 128, Z))
     act(X("ivt", 0, 128), X("pa", 0, 128))
     mm(X("pb", 0, 128), X("ivt", 0, 128), X("iff", 0, 128))
-    pick("pc", 0, "gcm", 0, "g8", 0, 8, "cm")
     for j in range(2):
         a, b = 1024 * j, 1024 * j + 1024
         tt(X("tw", a, b), IX("sw", Z + 16, "mate", 64 * j, 64 * j + 64), X("p0", a, b), OP.add)
     ts(X("ivi", 0, 128), X("pb", 0, 128), 64.0, OP.subtract)
     cp(X("iv16", 0, 128), X("ivi", 0, 128))
     for j in range(4):
-        o, i = X("yt", 512 * j, 512 * j + 512), IX("tw", V + 16, "iv16", 32 * j, 32 * j + 32)
+        o, i = X("p0", 512 * j, 512 * j + 512), IX("tw", V + 16, "iv16", 32 * j, 32 * j + 32)
         if j % 2 == 0:
             cp(o, i)
         else:
             act(o, i)
         dma("Y", "y%d" % j, T.y[:, 512 * j:512 * j + 512], [], o[0], o[1])
+    pick("pc", 0, "g1", 0, "g8", 0, 8, "cm")
     act(X("cmt", 0, 128), X("pc", 0, 128))
     mm(X("pd", 0, 128), X("cmt", 0, 128), X("iff", 0, 128))
     act(X("cmv", 0, 128), X("pd", 0, 128))

import math
from concourse.bass import DstId, RemoteDMATransfer
from concourse.mybir import AluOpType, ActivationFunctionType

OP = AluOpType
AF = ActivationFunctionType
V, C, Z = 2048, 96, 2432
F32, BF, I32, U16 = "float32", "bfloat16", "int32", "uint16"
WIDTHS = {
    F32: dict(nbf=256, col=128, jr=8, jb=8, ir=128, rg=128, rgam=128, aw=128, ownt=256, ownp=128, iff=128, g8=8, sel1f=8, vl=128,
              vz=128, w0s=128, dn=128, bd=128, hlf=256, h4=256, l4=256, beta=256, alph=256, stf=512, pif=256, t1=256, xf=2432,
              num=128, cn=128, off=128, ms=128, sp=2432, sb=384, g1=2048, p0=2048, sw=2448, sst=384, id64=2048, inv=4096,
              ivt=128, cmt=128, cmv=128, tw=2064, xb=384, gA=384, pB=384, bq=768, bqt=256),
    BF: dict(wsb=4096, xw=2448, ia=256, ic=256, nwa=256, nwb=256, ib=128, i128=64, blk=128, lt=128, tri=128, samg=128, pack=1024,
             src=512, lst=64, selg=24, sel4=16, sel1=8, nw=2432, bst=384, xst=384, xc=2048, wtb=2, bt=128, gb=8192, rh=256,
             wr=4096, sq=512, wm=8192, mq=512, zt=128, zl=128, np=256, np9=256, mlh=128, ml10=128, ww=1024, ar=256,
             mcode=128, tc=128, rep=128, rt=128, up=128, kc=128, one=128, thr=256, tq=128),
    I32: dict(bli=24, nbi=256, coli=16, li=256, sti=512, lj=256, yi=512, zi=512, ivi=128, bwi=48, nbw=4096, nbl=48),
    U16: dict(bl16=24, hl16=256, pl16=256, idx=512, mate=128, ms16=128, off16=128, iv16=128, nb16=256, bw16=24, nbb16=48),
}
PSUM = {"psw": 2048, "pa": 512, "pb": 512, "pc": 512, "pd": 512}
SCRATCH = {"snd": ("sbuf", [128, 4, 128], BF), "tg": ("sbuf", [128, 4, 128], BF)}
for _d in WIDTHS:
    for _n in WIDTHS[_d]:
        SCRATCH[_n] = ("sbuf", [128, WIDTHS[_d][_n]], _d)
for _n in PSUM:
    SCRATCH[_n] = ("psum", [128, PSUM[_n]], F32)
EXCH = ["name", "x", "gid", "code", "xs", "num", "s"]
LOADS = ["bl", "nb", "w", "x", "xc", "nbw", "wr", "y0", "y1", "y2", "y3", "cm"]
SEMAPHORES = ["cV", "cS", "cP", "cG"] + ["d_" + k for k in LOADS] + ["a_" + k for k in EXCH] + ["l_" + k for k in EXCH]
SHARE = {"gid": (1024, 1024), "names": (1024, 512), "r0": (1024, 768, 896, 640), "r1": (1024, 1024, 896, 832), "x": 1408}


def engine_plan(topo, src, cores):
    away = [d for d in cores if d != src and topo.chip(d) != topo.chip(src)]
    near = [d for d in cores if d != src and topo.chip(d) == topo.chip(src)]
    used, out = [], {}
    for group in (away, near):
        for i, d in enumerate(group):
            free = [e for e in topo.engines(src, d) if e not in used]
            n = 1
            while n * 2 <= len(free) // (len(group) - i) and n < 8:
                n *= 2
            out[d] = free[:n]
            used = used + out[d]
    return out


def rank_program(g, core, T, topo):
    r = T.rank_of(core)
    if r is None:
        return
    cores = [int(c) for c in T.cores]
    others = [d for d in range(len(cores)) if d != r]
    queue = {"V": g.vector, "S": g.scalar, "P": g.tensor, "G": g, "Y": g.sync}
    total, known, hist = {}, {q: {} for q in queue}, {}

    def deps(q, tag, regs, kind, need):
        for name, p0, p1, c0, c1 in regs:
            ps = name in PSUM
            for o, k, a0, a1, b0, b1 in hist.get(name, ()):
                cross = ps and o["q"] != q
                if kind == "r" and k == "r" and not cross:
                    continue
                if tag is not None and o["tag"] == tag and o["q"] == q:
                    continue
                if cross:
                    hit = c0 // 512 <= (b1 - 1) // 512 and b0 // 512 <= (c1 - 1) // 512
                else:
                    hit = c0 < b1 and b0 < c1 and p0 < a1 and a0 < p1
                if hit and (o["sem"] not in need or need[o["sem"]]["val"] < o["val"]):
                    need[o["sem"]] = o

    def note(o, outs, ins):
        for kind, regs in (("w", outs), ("r", ins)):
            for name, p0, p1, c0, c1 in regs:
                hist.setdefault(name, []).append((o, kind, p0, p1, c0, c1))

    def add(q, fn, outs, ins, sem=None, inc=1, tag=None, chain=True):
        need, kq = {}, known[q]
        deps(q, tag, ins, "r", need)
        deps(q, tag, outs, "w", need)
        for s, o in need.items():
            if kq.get(s, 0) >= o["val"] or any(p is not o and p["know"].get(s, 0) >= o["val"] for p in need.values()):
                continue
            queue[q].wait_ge(T.sem[s], o["val"])
            for k, v in o["know"].items():
                kq[k] = max(kq.get(k, 0), v)
        sem = sem or "c" + q
        total[sem] = total.get(sem, 0) + inc
        o = {"q": q if sem == "c" + q else q + sem, "tag": tag, "sem": sem, "val": total[sem], "know": dict(kq)}
        o["know"][sem] = total[sem]
        made = fn(queue[q])
        if chain:
            made.then_inc(T.sem[sem], inc)
        note(o, outs, ins)

    def X(name, c0, c1, step=1, p0=0, p1=128):
        ap = T[name][p0:p1, c0:c1] if step == 1 else T[name][p0:p1, c0:c1:step]
        return ap, [(name, p0, p1, c0, c1)]

    def X3(name, i0, i1, j0, j1):
        ap = T[name][:, i0:i1, j0:j1] if i1 - i0 > 1 else T[name][:, i0, j0:j1]
        return ap, [(name, 0, 128, i0 * 128 + j0, (i1 - 1) * 128 + j1)]

    def IX(win, b, offs, c, d, a=0):
        return T[win][:, a:b].indirect(T[offs][:, c:d]), [(win, 0, 128, a, b), (offs, 0, 128, c, d)]

    def col(j, p1=128):
        return X("col", j, j + 1, 1, 0, p1)

    def sc(s):
        return s[0] if isinstance(s, tuple) else s

    def rg(*xs):
        return [y for x in xs if isinstance(x, tuple) for y in x[1]]

    def tt(out, a, b, op, tag=None):
        add("V", lambda e: e.tensor_tensor(out=out[0], in0=a[0], in1=b[0], op=op), rg(out), rg(a, b), tag=tag)

    def ts(out, a, s1, op0, s2=None, op1=None, tag=None):
        if op1 is None:
            f = lambda e: e.tensor_scalar(out=out[0], in0=a[0], scalar1=sc(s1), scalar2=None, op0=op0)
        else:
            f = lambda e: e.tensor_scalar(out=out[0], in0=a[0], scalar1=sc(s1), scalar2=sc(s2), op0=op0, op1=op1)
        add("V", f, rg(out), rg(a, s1, s2), tag=tag)

    def cp(out, a, tag=None):
        add("V", lambda e: e.tensor_copy(out=out[0], in_=a[0]), rg(out), rg(a), tag=tag)

    def act(out, a, func=AF.Identity, bias=0.0, scale=1.0, tag=None):
        if isinstance(bias, float) and isinstance(scale, float) and bias == 0.0 and scale == 1.0:
            f = lambda e: e.activation(out=out[0], in_=a[0], func=func)
        else:
            f = lambda e: e.activation(out=out[0], in_=a[0], func=func, bias=sc(bias), scale=sc(scale))
        add("S", f, rg(out), rg(a, bias, scale), tag=tag)

    def mm(out, lhsT, rhs, start=True, stop=True, tag=None):
        add("P", lambda e: e.matmul(out=out[0], lhsT=lhsT[0], rhs=rhs[0], start=start, stop=stop), rg(out), rg(lhsT, rhs), tag=tag)

    def iota(out, pattern, base, cm, whole=False):
        if whole:
            f = lambda e: e.iota(out[0], pattern, base, cm)
        else:
            f = lambda e: e.iota(out[0], pattern, base, cm, allow_small_or_imprecise_dtypes=True)
        add("G", f, rg(out), [])

    def keep(out, a):
        add("G", lambda e: e.affine_select(out[0], a[0], [[1, 512]], OP.is_ge, 0.0, 0, 0), rg(out), rg(a))

    def dma(q, key, out_ap, outs, in_ap, ins):
        add(q, lambda e: e.dma_start(out=out_ap, in_=in_ap), outs, ins, sem="d_" + key, inc=16)

    plans = {c: engine_plan(topo, c, cores) for c in cores}

    def send(key, src, dst):
        parts, regs, n = [], [], 0
        for d in others:
            eng = plans[core][cores[d]]
            n += len(eng)
            a = topo.addr(cores[d])
            s = src(d)
            regs += s[1]
            parts.append(RemoteDMATransfer(dst_ids=[DstId(rid=a[0], pnc=a[1])], dma_engine_mask=sum(1 << e for e in eng),
                                           remote_sem=T.sem["a_" + key], srcs=[s[0]], dsts=[dst[0]]))
        add("G", lambda e: e.remote_dma_fused(parts, local_sem=T.sem["l_" + key]), [], regs, sem="l_" + key, inc=n, chain=False)

    def recv(key, regs):
        n = sum(len(plans[cores[q]][core]) for q in others)
        total["a_" + key] = n
        note({"q": "R", "tag": None, "sem": "a_" + key, "val": n, "know": {"a_" + key: n}}, regs, [])

    def ghosts(name):
        return [(name, 0, 128, V + C * q, V + C * q + C) for q in others]

    def pick(bank, c0, src, s0, sel, w0, w1, tag):
        n = 16 * (w1 - w0)
        for b in range(16):
            mm(X(bank, c0 + b, c0 + n, 16), X(src, s0 + b, s0 + V, 16), X(sel, w0, w1), tag=tag)

    def share(dst, a, win, w, offs, o, n):
        cp(X(dst, a, a + n), IX(win, w, offs, o, o + n // 16))
        act(X(dst, a + n, a + V), IX(win, w, offs, o + n // 16, o + 128))

    mine, LN2 = V + C * r, math.log(2.0)
    R4, KK, QB, QH, GM, WT, NQ, CV = (col(j) for j in (4, 5, 6, 7, 8, 9, 10, 11))
    MC, CX, CK, CJ = 16, 32, 36, 48
    dma("Y", "bl", T.bli[:, :], rg(X("bli", 0, 24)), T.bl[:, :], [])
    dma("S", "nb", T.nbi[:, :], rg(X("nbi", 0, 256)), T.nb[:, :], [])
    dma("Y", "w", T.wsb[0:8, :], rg(X("wsb", 0, 4096, 1, 0, 8)), T.w[:, :], [])
    dma("S", "x", T.xw[:, 0:V], rg(X("xw", 0, V)), T.x[:, :], [])
    dma("Y", "xc", T.xc[:, :], rg(X("xc", 0, V)), T.x[:, :], [])

    iota(X("coli", 0, 1), [[0, 1]], 0, 1, True)
    iota(X("ir", 0, 128), [[1, 128]], 0, 0)
    iota(X("jr", 0, 8), [[1, 4], [0, 2]], 4 * r, 0)
    iota(X("jb", 0, 8), [[0, 4], [1, 2]], 0, 0)
    iota(X("ia", 0, 256), [[0, 64], [1, 4]], 0, 0)
    iota(X("ic", 0, 256), [[1, 64], [0, 4]], 0, 0)
    iota(X("rg", 0, 128), [[1, 8], [0, 16]], 0, 0)
    for q in range(4):
        iota(X("rgam", 32 * q, 32 * q + 32), [[2, 2], [0, 8], [1, 2]], 0, 0)
    for q in range(4):
        iota(X("aw", 32 * q, 32 * q + 32), [[16, 2], [32, 4], [1, 4]], 0, -1)
    ts(X("coli", 1, 2), X("coli", 0, 1), 15, OP.bitwise_and)
    ts(X("coli", 2, 3), X("coli", 0, 1), 4, OP.logical_shift_right)
    cp(X("col", 0, 3), X("coli", 0, 3))
    ts(X("col", MC, MC + 16), X("ir", 0, 16), col(1), OP.is_equal)
    ts(X("ib", 0, 128), X("ir", 0, 128), col(0), OP.is_equal)
    ts(X("jr", 0, 8), X("jr", 0, 8), col(MC + 2), OP.mult)
    ts(X("jb", 0, 8), X("jb", 0, 8), col(MC + 3), OP.mult)
    tt(X("col", CJ, CJ + 8), X("jr", 0, 8), X("jb", 0, 8), OP.add)
    ts(X("nwa", 0, 256), X("ia", 0, 256), col(MC), OP.mult)
    ts(X("g8", 0, 8), X("ir", 0, 8), col(2), OP.is_equal)
    cp(X("bl16", 0, 24), X("bli", 0, 24))
    ts(X("nwb", 0, 256), X("ic", 0, 256), col(MC + 1), OP.mult)
    tt(X("nwb", 0, 256), X("nwa", 0, 256), X("nwb", 0, 256), OP.add)
    for j in range(8):
        o = X("nw", 256 * j, 256 * j + 256)
        if j % 3 == 1:
            act(o, X("nwb", 0, 256), AF.Identity, col(CJ + j))
        else:
            ts(o, X("nwb", 0, 256), col(CJ + j), OP.add)
    cp(X("bst", 0, 384), IX("nw", V, "bl16", 0, 24))
    send("name", lambda d: X("bst", C * d, C * d + C), X("nw", mine, mine + C))
    act(X("nw", mine, mine + C), IX("nw", V, "bl16", 6 * r, 6 * r + 6))

    for d in range(2):
        for b in range(16):
            mm(X(("pa", "pc")[d], b, 128, 16), X("wsb", d * V + b, d * V + V, 16, 0, 8), X("ib", 0, 8, 1, 0, 8), tag="wt")
    act(X("w0s", 0, 128), X("pa", 0, 128))
    act(X("xst", 0, 384), IX("xw", V, "bl16", 0, 24))
    send("x", lambda d: X("xst", C * d, C * d + C), X("xw", mine, mine + C))
    act(X("xw", mine, mine + C), IX("xw", V, "bl16", 6 * r, 6 * r + 6))
    recv("name", ghosts("nw"))
    recv("x", ghosts("xw"))
    cp(X("nbf", 0, 256), X("nbi", 0, 256))
    tt(X("dn", 0, 128), X("nbf", 128, 256), X("nbf", 0, 128), OP.subtract)
    tt(X("bt", 0, 128), X("pc", 0, 128), X("w0s", 0, 128), OP.is_gt)
    mm(X("pb", 0, 128), X("bt", 0, 128), X("ib", 0, 128))
    ts(col(60), col(MC), 16.0, OP.mult, col(MC + 2), OP.add)
    ts(col(61), col(MC + 3), 64.0, OP.mult, col(MC + 1), OP.add)
    tt(X("bd", 0, 128), X("pb", 0, 128), X("dn", 0, 128), OP.mult)
    tt(X("hlf", 0, 128), X("nbf", 0, 128), X("bd", 0, 128), OP.add)
    cp(X("hl16", 0, 128), X("hlf", 0, 128))
    tt(X("hlf", 128, 256), X("nbf", 128, 256), X("bd", 0, 128), OP.subtract)
    cp(X("hl16", 128, 256), X("hlf", 128, 256))
    for f in range(2):
        ts(X("selg", 8 * f, 8 * f + 8), X("g8", 0, 8), col(60 + f), OP.mult)
    ts(col(62), col(MC + 1), 4.0, OP.mult, col(MC), OP.add)
    ts(col(62), col(MC + 2), 512.0, OP.mult, col(62), OP.add)
    ts(col(62), col(MC + 3), 256.0, OP.mult, col(62), OP.add)
    ts(X("selg", 16, 24), X("g8", 0, 8), col(62), OP.mult)
    ts(X("coli", 3, 4), X("coli", 0, 1), 1, OP.logical_shift_right, 1, OP.bitwise_and)
    ts(X("coli", 4, 5), X("coli", 0, 1), 3, OP.bitwise_and)
    ts(X("coli", 5, 6), X("coli", 0, 1), 2, OP.logical_shift_right, 3, OP.bitwise_and)
    ts(X("coli", 6, 7), X("coli", 0, 1), 5, OP.logical_shift_right, 1, OP.bitwise_and)
    ts(X("coli", 7, 8), X("coli", 0, 1), 6, OP.logical_shift_right)
    ts(X("coli", 8, 9), X("coli", 0, 1), 4, OP.logical_shift_right, 1, OP.bitwise_and)
    cp(X("col", 3, 9), X("coli", 3, 9))
    ts(CV, R4, 2.0, OP.mult, QH, OP.add)
    ts(X("col", CX, CX + 4), X("ir", 0, 4), R4, OP.is_equal)
    ts(X("col", CK, CK + 4), X("ir", 0, 4), KK, OP.is_equal)

    for K in range(2):
        share("gb", K * V, "nw", Z, "hl16", K * 128, SHARE["gid"][K])
        pick("pa", K * 256, "gb", K * V, "selg", 0, 16, "gid")
    for K in range(2):
        for f in range(2):
            cp(X3("snd", 0, 4, 64 * f + K * 32, 64 * f + K * 32 + 32), X("pa", K * 256 + f * 128, K * 256 + f * 128 + 128), tag="snd")
    act(X("wtb", 0, 1), CV, AF.Exp, 0.0, 2 * LN2)
    send("gid", lambda d: X3("snd", d, d + 1, 0, 128), X3("tg", r, r + 1, 0, 128))
    for K in range(2):
        pick("pb", 256 + K * 128, "gb", K * V, "selg", 16, 24, "gid2")
    cp(X3("tg", r, r + 1, 0, 128), X3("snd", r, r + 1, 0, 128))
    recv("gid", [("tg", 0, 128, q * 128, q * 128 + 128) for q in others])
    for K in range(2):
        iota(X("ownt", 128 * K, 128 * K + 128), [[0, 8], [1, 16]], V * r, 16)
    for q in range(4):
        iota(X("ownp", 32 * q, 32 * q + 32), [[0, 2], [1, 4], [2048, 4]], 512 * q, 4)
    iota(X("kc", 0, 128), [[0, 128]], 8192, 0)
    iota(X("one", 0, 128), [[0, 128]], 1, 0)
    iota(X("xw", Z, Z + 16), [[0, 16]], 0, 0)
    iota(X("sw", Z, Z + 16), [[0, 16]], 0, 0)
    iota(X("tw", V, V + 16), [[0, 16]], 0, 0)
    iota(X("vl", 0, 128), [[16, 128]], V, 0)
    iota(X("nbw", 0, 4096), [[0, 4096]], 0, 0, True)
    iota(X("inv", 0, V), [[0, V]], V + 64, 0)
    iota(X("id64", 0, V), [[1, V]], 64, 0)
    for c in range(16):
        dma("Y", "wr", T.wr[c:128:16, :], [("wr", 16 * k + c, 16 * k + c + 1, 0, 4096) for k in range(8)], T.w[:, :],
            [("tg", 0, 128, 0, 512)])
    for k in range(8):
        dma("Y", "nbw", T.nbw[16 * k:16 * k + 1, :], [("nbw", 16 * k, 16 * k + 1, 0, 4096)], T.nb[16 * k:16 * k + 16, :], [])

    for x in range(4):
        ts(X("src", x * 128, x * 128 + 128), X("aw", 0, 128), float(-4 * x), OP.is_equal)
    act(X("i128", 0, 64), X("ib", 0, 64), AF.Identity, 0.0, 128.0)
    tt(X("lst", 0, 64), X("i128", 0, 64), X("ib", 64, 128), OP.add)
    for K in range(2):
        ts(col(80 + K), col(CK + K), 128.0, OP.mult, col(CK + 2 + K), OP.add)
        ts(X("sel4", 8 * K, 8 * K + 8), X("g8", 0, 8), col(80 + K), OP.mult)
    tt(col(63), col(MC), col(MC + 1), OP.add)
    ts(X("sel1", 0, 8), X("g8", 0, 8), col(63), OP.mult)
    cp(WT, X("wtb", 0, 1))
    ts(NQ, QB, 0.0, OP.is_equal)
    ts(col(64), GM, 2.0, OP.mult, col(3), OP.add)
    ts(X("iff", 0, 128), X("ir", 0, 128), col(0), OP.is_equal)
    ts(X("samg", 0, 128), X("rgam", 0, 128), col(64), OP.is_equal)
    ts(X("col", 84, 88), X("col", CK, CK + 4), WT, OP.mult, NQ, OP.mult)
    ts(X("col", 88, 92), X("col", CK, CK + 4), WT, OP.mult, QB, OP.mult)
    for j in range(8):
        act(X("pack", j * 128, j * 128 + 128), X("samg", 0, 128), AF.Identity, 0.0, col(84 + j))
    tt(X("rh", 0, 256), X("pb", 256, 512), X("ownt", 0, 256), OP.is_gt)
    for K in range(2):
        mm(X("pd", K * 128, K * 128 + 128), X("rh", K * 128, K * 128 + 128), X("ib", 0, 128))
    for K, n in ((0, "h4"), (1, "l4")):
        act(X(n, 0, 128), X("hlf", K * 128, K * 128 + 128), AF.Identity, -float(Z))
        act(X(n, 128, 256), X("pd", K * 128, K * 128 + 128), AF.Identity, -1.0)

    for q in [r] + others:
        mm(X("pc", q * 128, q * 128 + 128), X3("tg", q, q + 1, 0, 128), X("ib", 0, 128), tag="sq")
    cp(X("sq", 0, 512), X("pc", 0, 512))
    for q in range(4):
        for x in range(4):
            mm(X("psw", q * 512 + x, q * 512 + 512, 4), X("src", x * 128, x * 128 + 128), X("sq", q * 128, q * 128 + 128), tag="src")
    for K in range(2):
        for q in range(4):
            mm(X("pa", K * 128, K * 128 + 128, 1, 32 * q, 32 * q + 32), X("lst", 32 * K, 32 * K + 32), X("sq", q * 128, q * 128 + 128), tag="lst")
    cp(X("nb16", 0, 256), X("nbi", 0, 256))
    ts(X("blk", 0, 128), X("rg", 0, 128), col(2), OP.is_equal)
    ts(X("tri", 0, 128), X("ir", 0, 128), col(0), OP.is_gt)
    tt(X("lt", 0, 128), X("tri", 0, 128), X("blk", 0, 128), OP.mult)
    ts(X("sel1f", 0, 8), X("g8", 0, 8), col(MC), OP.mult)
    ts(X("bwi", 0, 24), X("bli", 0, 24), 4, OP.logical_shift_right)
    ts(X("bwi", 24, 48), X("bli", 0, 24), 15, OP.bitwise_and)
    ts(X("bwi", 24, 48), X("bwi", 24, 48), 256.0, OP.mult)
    tt(X("bwi", 0, 24), X("bwi", 0, 24), X("bwi", 24, 48), OP.add)
    cp(X("bw16", 0, 24), X("bwi", 0, 24))
    for h in range(2):
        for x in range(4):
            o, i = X("wm", x * 2048 + h * 1024, x * 2048 + h * 1024 + 1024), X("psw", h * 1024, h * 1024 + 1024)
            if h == 0:
                ts(o, i, col(CX + x), OP.mult)
            else:
                act(o, i, AF.Identity, 0.0, col(CX + x))
    cp(X("pl16", 0, 256), X("pa", 0, 256))

    def places(a, b):
        act(X("mq", a, b), X("stf", a, b), AF.Exp, 0.0, -2 * LN2)

    for K in range(2):
        share("gb", K * V, "wm", 8192, "pl16", K * 128, SHARE["names"][K])
        if K == 0:
            cp(X("li", 0, 256), X("pa", 0, 256))
            for k in range(2):
                ts(X("sti", k * 128, k * 128 + 128), X3("tg", 0, 4, k * 32, k * 32 + 32), 0.125, OP.mult, -0.4375, OP.add)
            cp(X("stf", 0, 256), X("sti", 0, 256))
            pick("pb", 0, "gb", 0, "sel4", 0, 16, "names")
    places(0, 256)
    act(X("vl", 0, 128), X("vl", 0, 128), AF.Identity, col(1))
    act(X("vz", 0, 128), X("vl", 0, 128), AF.Identity, -float(V + Z))
    tt(X("zt", 0, 128), X("pb", 0, 128), X("ownp", 0, 128), OP.is_equal)

    def pack_z(parts, before, between):
        for i, p in enumerate(parts):
            mm(X("pa", 0, 128), p, X("ib", 0, 128), i == 0, i == len(parts) - 1, tag="zl")
        before()
        cp(X("zl", 0, 128), X("pa", 0, 128))
        for h in range(2):
            for x in range(4):
                j = h * 4 + x
                mm(X("psw", h * 512 + x, h * 512 + 512, 4), X("pack", j * 128, j * 128 + 128), X("zl", 0, 128), tag="pack")
        between()
        cp(X("ww", 0, 512), X("psw", 0, 512))
        act(X("ww", 512, 1024), X("psw", 512, 1024))

    def lists():
        tt(X("np", 0, 128), X("pb", 128, 256), X("ownp", 0, 128), OP.not_equal)
        ts(X("li", 0, 256), X("li", 0, 256), 1023, OP.bitwise_and)
        cp(X("idx", 0, 256), X("li", 0, 256))

    pack_z([X("zt", 0, 128)], lambda: cp(X("pif", 0, 128), X("pb", 0, 128)), lists)
    pick("pd", 0, "gb", V, "sel4", 0, 16, "names")
    cp(X("mcode", 0, 128), X("zt", 0, 128))

    def ask(L, n):
        share("gb", L * V, "ww", 1024, "idx", L * 128, n)

    def answer(L):
        bank, c0 = ("pc", "pd")[L // 2], (L % 2) * 128
        if L == 3:
            mm(X(bank, c0, c0 + 128), X("kc", 0, 128), X("one", 0, 128), True, False, tag="zz")
        for b in range(16):
            mm(X(bank, c0 + b, c0 + 128, 16), X("gb", L * V + b, L * V + V, 16), X("sel1", 0, 8), L != 3, L != 3 or b == 15, tag="zz")

    def bits(H):
        a, bank = H * 256, ("pc", "pd")[H]
        tt(X("yi", a, a + 256), X(bank, 0, 256), X("mq", a, a + 256), OP.mult)
        ts(X("zi", a, a + 256), X("yi", a, a + 256), 1, OP.bitwise_and)

    def border_lists(d):
        for b in range(16):
            mm(X("pa", d * 128 + b, d * 128 + 128, 16, 0, 24), X("bq", d * 384 + b, d * 384 + 384, 16), X("sel1f", 0, 8), tag="bq")

    ARH, ARL = X("ar", 0, 128), X("ar", 128, 256)
    for t in range(2):
        n = SHARE["r%d" % t]
        if t == 1:
            border_lists(0)
        ask(0, n[0])
        if t == 0:
            cp(X("pif", 128, 256), X("pd", 0, 128))
            for K in range(2):
                mm(X("pb", K * 128, K * 128 + 128), X("pif", K * 128, K * 128 + 128), X("iff", 0, 128))
            tt(X("np", 128, 256), X("pd", 128, 256), X("ownp", 0, 128), OP.not_equal)
            tt(X("mlh", 0, 128), X("pd", 0, 128), X("ownp", 0, 128), OP.is_equal)
        answer(0)
        ask(1, n[1])
        if t == 0:
            cp(X("lj", 0, 256), X("pb", 0, 256))
            ts(X("lj", 0, 256), X("lj", 0, 256), 1023, OP.bitwise_and)
            cp(X("idx", 256, 512), X("lj", 0, 256))
            act(X("np9", 0, 256), X("np", 0, 256), AF.Identity, 0.0, 9.0)
            act(X("ml10", 0, 128), X("mlh", 0, 128), AF.Identity, 0.0, 10.0)
            ts(X("sti", 256, 512), X("pif", 0, 256), 1.0 / 1024, OP.mult, -0.5 + 1.0 / 2048, OP.add)
        answer(1)
        if t == 0:
            tt(X("stf", 256, 512), X("sti", 256, 512), X("np9", 0, 256), OP.max)
            tt(X("stf", 384, 512), X("stf", 384, 512), X("ml10", 0, 128), OP.max)
        ask(2, n[2])
        answer(2)
        if t == 0:
            places(256, 512)
        ask(3, n[3])
        answer(3)
        bits(0)
        tt(X("tq", 0, 128), X("zi", 0, 128), X("zt", 0, 128), OP.is_le)
        tt(X("thr", 0, 128), X("zi", 0, 128), X("zt", 0, 128), OP.max)
        tt(X("thr", 128, 256), X("zi", 128, 256), X("tq", 0, 128), OP.max)
        cp(X("bq", 384 * t, 384 * t + 384), IX("nbw", 4096, "bw16", 0, 24, 128 * t))
        bits(1)
        tt(X("ar", 0, 256), X("zi", 256, 512), X("thr", 0, 256), OP.is_gt)
        if t == 0:
            def more():
                tt(X("zt", 0, 128), X("zt", 0, 128), ARH, OP.add)
                tt(X("zt", 0, 128), X("zt", 0, 128), ARL, OP.add)
            pack_z([X("zt", 0, 128), ARH, ARL], lambda: None, more)
        tt(X("mcode", 0, 128), X("mcode", 0, 128), ARH, OP.add)
        tt(X("mcode", 0, 128), X("mcode", 0, 128), ARL, OP.subtract)
    border_lists(1)
    act(X("bqt", 0, 256, 1, 0, 24), X("pa", 0, 256, 1, 0, 24), AF.Silu, 64.0)
    send("code", lambda d: X("mcode", 32 * d, 32 * d + 32), X("tc", 32 * r, 32 * r + 32))
    cp(X("tc", 32 * r, 32 * r + 32), X("mcode", 32 * r, 32 * r + 32))
    recv("code", [("tc", 0, 128, 32 * q, 32 * q + 32) for q in others])

    tt(X("beta", 0, 256), X("h4", 0, 256), X("l4", 0, 256), OP.add)
    ts(X("beta", 0, 256), X("beta", 0, 256), 0.5, OP.mult)
    tt(X("alph", 0, 256), X("h4", 0, 256), X("beta", 0, 256), OP.subtract)
    for d in range(2):
        act(X("gb", V + 384 * d, V + 384 * d + 384), IX("wr", V + V * d, "bl16", 0, 24, V * d))
    for d in range(2):
        mm(X("pc", 256 + 24 * d, 280 + 24 * d), X("bqt", d * 128, d * 128 + 128, 1, 0, 24), X("iff", 0, 24, 1, 0, 24))

    mm(X("pc", 0, 128), X("tc", 0, 128), X("ib", 0, 128))

    def quad(a):
        tt(X("t1", a, a + 128), X("beta", a, a + 128), X("pc", 0, 128), OP.mult)
        tt(X("t1", a, a + 128), X("t1", a, a + 128), X("alph", a, a + 128), OP.add)
        tt(X("t1", a, a + 128), X("t1", a, a + 128), X("pc", 0, 128), OP.mult)

    for j in range(4):
        mm(X("psw", 512 * j, 512 * j + 512), X("ib", 0, 128), X("wr", V + 512 * j, V + 512 * j + 512))
    quad(0)
    ts(X("mate", 0, 128), X("t1", 0, 128), float(Z), OP.add)
    nx = SHARE["x"]
    tt(X("xf", 0, nx), IX("xw", Z + 16, "mate", 0, nx // 16), X("xc", 0, nx), OP.add)
    for i, (bank, a, b) in enumerate((("pa", nx, nx + 512), ("pb", nx + 512, V))):
        act(X("gb", a - nx, b - nx), IX("xw", Z + 16, "mate", a // 16, b // 16))
        mm(X(bank, 0, b - a), X("ib", 0, 128), X("xc", a, b), True, False, tag="gx")
        mm(X(bank, 0, b - a), X("ib", 0, 128), X("gb", a - nx, b - nx), False, True, tag="gx")
    for bank, a, b in (("pa", nx, nx + 512), ("pb", nx + 512, V)):
        act(X("xf", a, b), X(bank, 0, b - a))
    mm(X("pb", 0, 384), X("ib", 0, 128), X("gb", V + 384, V + 768))
    cp(X("xb", 0, 192), IX("xf", V, "bl16", 0, 12))
    act(X("xb", 192, 384), IX("xf", V, "bl16", 12, 24))
    send("xs", lambda d: X("xb", C * d, C * d + C), X("xf", mine, mine + C))
    act(X("xf", mine, mine + C), X("xb", C * r, C * r + C))
    recv("xs", ghosts("xf"))

    quad(128)
    ts(X("rep", 0, 128), X("t1", 128, 256), 1.0, OP.add)
    mm(X("pd", 0, 128), X("rep", 0, 128), X("ib", 0, 128))
    ts(X("nbl", 0, 48), X("pc", 256, 304), 64.0, OP.subtract)
    cp(X("nbb16", 0, 48), X("nbl", 0, 48))
    tt(X("ms", 0, 128), X("vz", 0, 128), X("t1", 0, 128), OP.subtract)
    tt(X("ms", 0, 128), X("ms", 0, 128), X("rep", 0, 128), OP.mult)
    tt(X("ms", 0, 128), X("ms", 0, 128), X("t1", 0, 128), OP.add)
    ts(X("ms16", 0, 128), X("ms", 0, 128), float(Z), OP.add)
    act(X("rt", 0, 128), X("pd", 0, 128))
    mm(X("pd", 128, 256), X("rt", 0, 128), X("tri", 0, 128))
    act(X("up", 0, 128), X("pd", 128, 256))
    mm(X("pd", 0, 128), X("blk", 0, 128), X("up", 0, 128), True, False, tag="num")
    mm(X("pd", 0, 128), X("lt", 0, 128), X("rep", 0, 128), False, True, tag="num")
    act(X("num", 0, 128), X("pd", 0, 128))
    act(X("cn", 0, 128), X("pd", 0, 128), AF.Identity, float(V * r))
    tt(X("off", 0, 128), X("num", 0, 128), X("vl", 0, 128), OP.subtract)
    tt(X("off", 0, 128), X("off", 0, 128), X("rep", 0, 128), OP.mult)
    tt(X("off", 0, 128), X("off", 0, 128), X("vl", 0, 128), OP.add)
    cp(X("off16", 0, 128), X("off", 0, 128))

    def SP(c):
        return X("sp", c, V, 16)[0], [("sp%d" % c, 0, 128, 0, 128)]

    def numbers(offs, c, d, b):
        ap, regs = IX("sp", b, offs, c, d)
        return ap, regs + [y for k in range(16) for y in SP(k)[1]]

    for c in range(16):
        if c < 4:
            ts(SP(c), X("cn", 0, 128), col(MC + c), OP.mult)
        else:
            act(SP(c), X("cn", 0, 128), AF.Identity, 0.0, col(MC + c))
    act(X("sb", 0, 384), numbers("bl16", 0, 24, V))
    send("num", lambda d: X("sb", C * d, C * d + C), X("sp", mine, mine + C))
    act(X("sp", mine, mine + C), X("sb", C * r, C * r + C))
    recv("num", ghosts("sp"))

    def invert(j):
        o = IX("inv", 4096, "off16", 32 * j, 32 * j + 32)
        i = X("id64", 512 * j, 512 * j + 512)
        add("S", lambda e: e.activation(out=o[0], in_=i[0], func=AF.Silu), [("inv", 0, 128, 0, 4096)],
            rg(i) + [("off16", 0, 128, 32 * j, 32 * j + 32)])

    def times_w0(a, b):
        tt(X("p0", a, b), IX("xf", Z, "nb16", a // 16, b // 16), X("wr", a, b), OP.mult)

    act(X("gA", 0, 384), IX("xf", Z, "nbb16", 24, 48))
    tt(X("pB", 0, 384), IX("xf", Z, "nbb16", 0, 24), X("gb", V, V + 384), OP.mult)
    times_w0(0, 512)
    tt(X("pb", 0, 384), X("gA", 0, 384), X("pb", 0, 384), OP.mult)
    tt(X("sst", 0, 384), X("pB", 0, 384), X("pb", 0, 384), OP.add)
    send("s", lambda d: X("sst", C * d, C * d + C), X("sw", mine, mine + C))
    recv("s", ghosts("sw"))

    for j in range(4):
        a, b = 512 * j, 512 * j + 512
        act(X("g1", a, b), IX("xf", Z, "nb16", 128 + 32 * j, 160 + 32 * j))
        if j > 0:
            invert(j - 1)
    invert(3)
    act(X("sw", mine, mine + C), X("sst", C * r, C * r + C))
    for j in range(4):
        a, b = 512 * j, 512 * j + 512
        if j > 0:
            times_w0(a, b)
        tt(X("psw", a, b), X("g1", a, b), X("psw", a, b), OP.mult)
        tt(X("sw", a, b), X("p0", a, b), X("psw", a, b), OP.add)
        keep(X("p0", a, b), X("sw", a, b))
    pick("pa", 0, "inv", 0, "sel1f", 0, 8, "inv")
    act(X("g1", 0, V), numbers("ms16", 0, 128, Z))
    act(X("ivt", 0, 128), X("pa", 0, 128))
    mm(X("pb", 0, 128), X("ivt", 0, 128), X("iff", 0, 128))
    for j in range(2):
        a, b = 1024 * j, 1024 * j + 1024
        tt(X("tw", a, b), IX("sw", Z + 16, "mate", 64 * j, 64 * j + 64), X("p0", a, b), OP.add)
    ts(X("ivi", 0, 128), X("pb", 0, 128), 64.0, OP.subtract)
    cp(X("iv16", 0, 128), X("ivi", 0, 128))
    for j in range(4):
        o, i = X("p0", 512 * j, 512 * j + 512), IX("tw", V + 16, "iv16", 32 * j, 32 * j + 32)
        if j % 2 == 0:
            cp(o, i)
        else:
            act(o, i)
        dma("Y", "y%d" % j, T.y[:, 512 * j:512 * j + 512], [], o[0], o[1])
    pick("pc", 0, "g1", 0, "g8", 0, 8, "cm")
    act(X("cmt", 0, 128), X("pc", 0, 128))
    mm(X("pd", 0, 128), X("cmt", 0, 128), X("iff", 0, 128))
    act(X("cmv", 0, 128), X("pd", 0, 128))
    dma("Y", "cm", T.cm[:, :], [], T.cmv[:, :], rg(X("cmv", 0, 128)))
    for s, v in total.items():
        if known["G"].get(s, 0) < v:
            g.wait_ge(T.sem[s], v)
